import numpy as np
import ml_dtypes


def mxq(x, axis, fmt="e4m3"):
    dtype, down = {"e4m3": (ml_dtypes.float8_e4m3fn, 7), "e5m2": (ml_dtypes.float8_e5m2, 14)}[fmt]
    v = np.moveaxis(np.asarray(x, np.float32).astype(ml_dtypes.bfloat16).astype(np.float64), axis, -1)
    blocks = v.reshape(v.shape[:-1] + (-1, 32))
    amax = np.abs(blocks).max(-1, keepdims=True)
    byte = np.maximum(np.where(amax > 0, np.frexp(amax)[1] - 1 + 127, 0) - down, 1)
    scale = np.exp2(byte - 127.0)
    codes = (blocks / scale).astype(np.float32).astype(dtype).astype(np.float64)
    return np.moveaxis((codes * scale).reshape(v.shape), -1, axis)


WIDE = False


def mx_kscale(k):
    if not WIDE:
        return np.ones(k)
    levels = np.array([10, -10, 5, -5, 0])
    if k % 512:
        return np.exp2(np.random.permutation(np.resize(levels, k // 32))).repeat(32)
    a = np.empty((k // 512, 16))
    for p in range(k // 512):
        a[p, :8] = np.random.permutation(np.resize(levels, 8))
        for g in range(8):
            far = levels[np.abs(levels - a[p, g]) >= 10]
            a[p, g + 8] = far[np.random.randint(len(far))]
    return np.exp2(a.ravel()).repeat(32)


def f64(x):
    return np.asarray(x).astype(np.float64)


def striped(idx):
    return np.tile(idx.reshape(-1, 16).T, (8, 1)).astype(np.uint16)


def unstriped(offs):
    return offs[:16].T.reshape(-1).astype(np.int64)


E2M1 = np.array([0.0, 0.5, 1.0, 1.5, 2.0, 3.0, 4.0, 6.0, -0.0, -0.5, -1.0, -1.5, -2.0, -3.0, -4.0, -6.0])


def pack_fp4(w):
    k, n = w.shape
    w = f64(np.asarray(w, np.float32).astype(ml_dtypes.bfloat16)).reshape(k // 32, 32, n)
    amax = np.abs(w).max(1)
    mant, ex = np.frexp(amax / 6.0)
    byte = np.clip(np.where(amax > 0, np.where(mant > 0.5, ex, ex - 1) + 127, 1), 1, 254)
    scaled = (w * np.exp2(127.0 - byte)[:, None, :]).reshape(k, n).astype(np.float32)
    c = np.ascontiguousarray(scaled.reshape(k // 512, 128, 4, n).transpose(0, 1, 3, 2)).astype(ml_dtypes.float4_e2m1fn).view(np.uint8) & 0xF
    words = (c[..., 0::2] | (c[..., 1::2] << 4)).reshape(k // 512, 128, 2 * n)
    return np.ascontiguousarray(words), np.ascontiguousarray(byte.astype(np.uint8).reshape(k // 512, 16, n))


def unpack_fp4(words, scales):
    g, _, n = scales.shape
    words = np.ascontiguousarray(words).reshape(g, 128, n, 2)
    nib = np.empty((g, 128, n, 4), np.uint8)
    nib[..., 0::2] = words & 0xF
    nib[..., 1::2] = words >> 4
    vals = E2M1[nib] * np.repeat(np.exp2(scales.astype(np.float64) - 127.0), 8, axis=1)[..., None]
    return vals.transpose(0, 1, 3, 2).reshape(g * 512, n)


def silu(v):
    return v / (1.0 + np.exp(-np.maximum(v, -700.0)))


K, T, S, H, N = 512, 2048, 1024, 512, 128
P = 2 ** 7


def setup_inputs():
    n = np.random.standard_normal
    s = mx_kscale(K)[:, None]
    u = mx_kscale(H)
    packed_w2 = pack_fp4(n((H, N)) / np.sqrt(H) / u[:, None])
    return {
        "xT": (n((K, T)) * s).astype(np.float32),
        "gate": np.tile(np.random.uniform(0.2, 1.0, T), (P, 1)).astype(np.float32),
        "w1": (n((K, H)) / np.sqrt(K) / s * u).astype(np.float32),
        "w2_words": packed_w2[0],
        "w2_scales": packed_w2[1],
        "offs": striped(np.random.permutation(T)[:S]),
    }


def reference(xT, gate, w1, w2_words, w2_scales, offs):
    xq = mxq(f64(xT)[:, unstriped(offs)], 0, "e4m3")
    h = silu(mxq(f64(w1), 0, "e4m3").T @ xq)
    y = unpack_fp4(w2_words, w2_scales).T @ mxq(h, 0, "e4m3")
    g = f64(gate)[:1][:, unstriped(offs)]
    out = np.zeros((N, T))
    out[:, unstriped(offs)] = y * g
    return out

@@ -1,0 +1,207 @@
+from contextlib import ExitStack
+
+import concourse.mybir as mybir
+from concourse.masks import make_identity
+
+K, T, S, H, N = 512, 2048, 1024, 512, 128
+FLOPS = 2 * K * H * S + 2 * H * N * S
+BYTES = 4 * K * T + 4 * T + 4 * K * H + 128 * 256 + 16 * 128 + 2 * 128 * 64 + 4 * N * T
+
+F32 = mybir.dt.float32
+BF16 = mybir.dt.bfloat16
+U32 = mybir.dt.uint32
+I32 = mybir.dt.int32
+U16 = mybir.dt.uint16
+U8 = mybir.dt.uint8
+FP8X4 = mybir.dt.float8_e4m3fn_x4
+FP4X4 = mybir.dt.float4_e2m1fn_x4
+SILU = mybir.ActivationFunctionType.Silu
+MULT = mybir.AluOpType.mult
+
+P = 128
+CH = 256
+NCH = S // CH
+LOADS = [[512, 512, 512, 512], [512, 512, 512, 384, 128]]
+
+
+def tile_picked_modgate_mlpsilu_l_kernel(tc, xT, gate, w1, w2_words, w2_scales, offs, out):
+    nc = tc.nc
+    with ExitStack() as ctx:
+        keep = ctx.enter_context(tc.tile_pool(name="keep", bufs=1))
+        banks = ctx.enter_context(tc.psum_pool(name="banks", bufs=6))
+        ybanks = ctx.enter_context(tc.psum_pool(name="ybanks", bufs=2))
+
+        offsets = keep.tile([P, S // 16], U16, name="offsets")
+        gcol = keep.tile([P, 16], F32, name="gcol")
+        nc.scalar.dma_start(out=gcol[:], in_=gate[0, :].rearrange("(p b) -> p b", b=16))
+
+        warm = keep.tile([P, 2], F32, name="warm")
+        nc.vector.memset(warm[:], 0.0)
+        nc.scalar.activation(warm[:, 1:2], warm[:, 0:1], SILU)
+
+        x4 = xT.rearrange("(p j) w -> p j w", j=4)
+        raws = {}
+        for pair in range(2):
+            c0 = 0
+            for i, w in enumerate(LOADS[pair]):
+                raw = keep.tile([P, 2, w], F32, name=f"raw{pair}_{i}")
+                nc.sync.dma_start(out=raw[:], in_=x4[:, 2 * pair : 2 * pair + 2, c0 : c0 + w])
+                raws[pair, i] = (raw, c0, w)
+                if pair == 0 and i == 0:
+                    nc.sync.dma_start(offsets[:], offs)
+                c0 = c0 + w
+        w14 = w1.rearrange("(p j) c -> p j c", j=4)
+        wraw = []
+        for half in range(2):
+            wr = keep.tile([P, 4, 256], F32, name=f"wraw{half}")
+            nc.sync.dma_start(out=wr[:], in_=w14[:, :, 256 * half : 256 * half + 256])
+            wraw.append(wr)
+        w2w = keep.tile([P, 256], U8, name="w2w", align_bytes=64)
+        nc.sync.dma_start(out=w2w[:].bitcast(I32), in_=w2_words[0].bitcast(I32))
+        w2s = keep.tile([P, 128], U8, name="w2s", align_bytes=64)
+        nc.vector.memset(w2s[:].bitcast(I32), 0)
+        for q in range(4):
+            nc.sync.dma_start(out=w2s[32 * q : 32 * q + 4, :].bitcast(I32), in_=w2_scales[0, 4 * q : 4 * q + 4, :].bitcast(I32))
+
+        ident = keep.tile([P, P], F32, name="ident")
+        make_identity(nc, ident[:])
+        window = keep.tile([P, T], F32, name="window")
+        nc.gpsimd.memset(window[:], 0.0)
+
+        shared = keep.tile([P, T + 2 * CH], F32, name="shared", align_bytes=64)
+        gwin = shared[:, 0:T]
+        for q in range(4):
+            bank = banks.tile([P, 4, P], F32, name="bank")
+            for r in range(4):
+                b = 4 * q + r
+                nc.tensor.transpose(bank[:, r, :], gcol[:, b : b + 1].to_broadcast([P, P]), ident[:])
+            nc.vector.tensor_copy(
+                out=gwin.rearrange("i (p q r) -> i q p r", q=4, r=4)[:, q],
+                in_=bank[:].rearrange("i r p -> i p r"),
+            )
+        gsel = keep.tile([P, S], F32, name="gsel")
+        for c in range(NCH):
+            nc.vector.tensor_copy(out=gsel[:, c * CH : (c + 1) * CH], in_=gwin.indirect(offsets[:, c * CH // 16 : (c + 1) * CH // 16]))
+
+        xpair = [keep.tile([P, 2 * T], BF16, name=f"xpair{pair}") for pair in range(2)]
+        xg23 = keep.tile([P, 8 * CH], BF16, name="xg23", align_bytes=64)
+        xg = [shared[:, 0 : 2 * CH].bitcast(BF16), shared[:, 2 * CH : 4 * CH].bitcast(BF16), xg23[:, 0 : 4 * CH], xg23[:, 4 * CH : 8 * CH]]
+        g23 = [shared[:, T - 2 * CH : T].bitcast(U32), shared[:, T : T + 2 * CH].bitcast(U32)]
+        g23_both = shared[:, T - 2 * CH : T + 2 * CH].bitcast(U32).rearrange("p (u n) -> p n u", u=2)
+
+        def gather23(pair):
+            nc.vector.tensor_copy(out=g23[pair], in_=xpair[pair][:].bitcast(U32).indirect(offsets[:, 2 * CH // 16 : 4 * CH // 16]))
+
+        def cast(engine_copy, pair, i, a, b):
+            raw, c0, w = raws[pair, i]
+            engine_copy(
+                out=xpair[pair][:, 2 * (c0 + a) : 2 * (c0 + b)].rearrange("p (c j) -> p c j", j=2),
+                in_=raw[:, :, a:b].rearrange("p j c -> p c j"),
+            )
+
+        def gather(pair, c):
+            nc.vector.tensor_copy(
+                out=xg[c].bitcast(U32).rearrange("p (n u) -> p n u", u=2)[:, :, pair],
+                in_=xpair[pair][:].bitcast(U32).indirect(offsets[:, c * CH // 16 : (c + 1) * CH // 16]),
+            )
+
+        for i, w in enumerate(LOADS[0]):
+            cast(nc.vector.tensor_copy if i == 0 else nc.scalar.copy, 0, i, 0, w)
+        gather(0, 0)
+        gather(0, 1)
+        gather23(0)
+        for i, w in enumerate(LOADS[1]):
+            cast(nc.scalar.copy, 1, i, 0, w)
+
+        xcodes = [keep.tile([P, CH], U32, name=f"xcodes{c}", align_bytes=64) for c in range(NCH)]
+        xscales = [keep.tile([P, CH], U8, name=f"xscales{c}", align_bytes=64) for c in range(NCH)]
+
+        def quant_x(c):
+            nc.vector.quantize_mx(out=xcodes[c][:].bitcast(FP8X4), scales=xscales[c][:], in_=xg[c])
+
+        wgrp0 = keep.tile([P, 1024], BF16, name="wgrp0", align_bytes=64)
+        wgrp = [wgrp0[:], shared[:, T : T + 2 * CH].bitcast(BF16)]
+        wcodes = keep.tile([P, H], U32, name="wcodes", align_bytes=64)
+        wscales = keep.tile([P, H], U8, name="wscales", align_bytes=64)
+
+        def cast_w(half):
+            nc.scalar.copy(
+                out=wgrp[half].rearrange("p (t m j) -> p m t j", t=4, j=4),
+                in_=wraw[half][:].rearrange("p j (m t) -> p m t j", t=4),
+            )
+
+        def quant_w(half):
+            for t in range(4):
+                cols = slice(128 * t + 64 * half, 128 * t + 64 * half + 64)
+                nc.vector.quantize_mx(out=wcodes[:, cols].bitcast(FP8X4), scales=wscales[:, cols], in_=wgrp[half][:, 256 * t : 256 * t + 256])
+
+        cast_w(0)
+        cast_w(1)
+        gather(1, 0)
+        gather(1, 1)
+        quant_x(0)
+        quant_w(0)
+        quant_w(1)
+        quant_x(1)
+        gather23(1)
+        nc.vector.tensor_copy(out=xg23[:].bitcast(U32).rearrange("p (n u) -> p n u", u=2), in_=g23_both)
+        quant_x(2)
+        quant_x(3)
+
+        hb = [keep.tile([P, 4 * CH], BF16, name=f"hb{c}", align_bytes=64) for c in range(NCH)]
+        hcodes = [keep.tile([P, CH], U32, name=f"hcodes{c}", align_bytes=64) for c in range(NCH)]
+        hscales = [keep.tile([P, CH], U8, name=f"hscales{c}", align_bytes=64) for c in range(NCH)]
+        ysb = [keep.tile([P, CH], F32, name=f"ysb{c}") for c in range(NCH)]
+
+        def layer1(c):
+            for s in range(CH // P):
+                cols = slice(s * P, (s + 1) * P)
+                bank = banks.tile([P, 4, P], F32, name="bank")
+                for t in range(4):
+                    wc = slice(t * P, (t + 1) * P)
+                    nc.tensor.matmul_mx(
+                        out=bank[:, t, :],
+                        lhsT=wcodes[:, wc].bitcast(FP8X4),
+                        lhsT_scale=wscales[:, wc],
+                        rhs=xcodes[c][:, cols].bitcast(FP8X4),
+                        rhs_scale=xscales[c][:, cols],
+                        start=True,
+                        stop=True,
+                    )
+                nc.scalar.activation(
+                    hb[c][:, 4 * P * s : 4 * P * (s + 1)].rearrange("p (n t) -> p n t", t=4),
+                    bank[:].rearrange("p t n -> p n t"),
+                    SILU,
+                )
+
+        def layer2(c):
+            nc.vector.quantize_mx(out=hcodes[c][:].bitcast(FP8X4), scales=hscales[c][:], in_=hb[c][:])
+            yb = ybanks.tile([P, CH], F32, name="yb")
+            nc.tensor.matmul_mx(
+                out=yb[:],
+                lhsT=w2w[:].bitcast(FP4X4),
+                lhsT_scale=w2s[:],
+                rhs=hcodes[c][:].bitcast(FP8X4),
+                rhs_scale=hscales[c][:],
+                start=True,
+                stop=True,
+            )
+            nc.scalar.copy(out=ysb[c][:], in_=yb[:])
+
+        def scatter(c):
+            nc.vector.tensor_tensor(
+                window[:].indirect(offsets[:, c * CH // 16 : (c + 1) * CH // 16]),
+                ysb[c][:],
+                gsel[:, c * CH : (c + 1) * CH],
+                MULT,
+            )
+
+        layer1(0)
+        for c in range(NCH):
+            layer2(c)
+            if c + 1 < NCH:
+                layer1(c + 1)
+            if c > 0:
+                scatter(c - 1)
+        scatter(NCH - 1)
+        nc.sync.dma_start(out=out, in_=window[:])

@@ -21,35 +21,37 @@ MULT = mybir.AluOpType.mult
 P = 128
 CH = 256
 NCH = S // CH
-LOADS = [[512, 512, 512, 512], [512, 512, 512, 384, 128]]
+LOADS = [[(1024, 1024), (0, 1024)], [(1024, 1024), (0, 1024)]]
+SPARE = 8
 
 
 def tile_picked_modgate_mlpsilu_l_kernel(tc, xT, gate, w1, w2_words, w2_scales, offs, out):
     nc = tc.nc
     with ExitStack() as ctx:
         keep = ctx.enter_context(tc.tile_pool(name="keep", bufs=1))
-        banks = ctx.enter_context(tc.psum_pool(name="banks", bufs=6))
+        banks = ctx.enter_context(tc.psum_pool(name="banks", bufs=3))
         ybanks = ctx.enter_context(tc.psum_pool(name="ybanks", bufs=2))
 
         offsets = keep.tile([P, S // 16], U16, name="offsets")
         gcol = keep.tile([P, 16], F32, name="gcol")
-        nc.scalar.dma_start(out=gcol[:], in_=gate[0, :].rearrange("(p b) -> p b", b=16))
+        nc.sync.dma_start(out=gcol[:], in_=gate[0, :].rearrange("(p b) -> p b", b=16))
 
-        warm = keep.tile([P, 2], F32, name="warm")
-        nc.vector.memset(warm[:], 0.0)
-        nc.scalar.activation(warm[:, 1:2], warm[:, 0:1], SILU)
+        tables = keep.tile([P, 3 * T - SPARE], F32, name="tables")
+        gwin = tables[:, 0:T]
+        xpair = [tables[:, T - SPARE : 2 * T - SPARE], tables[:, 2 * T - SPARE : 3 * T - SPARE]]
+        warm = keep.tile([P, 1], F32, name="warm")
+        nc.vector.memset(xpair[1][:, 0:SPARE], 0.0)
+        nc.scalar.activation(warm[:], xpair[1][:, 0:1], SILU)
 
         x4 = xT.rearrange("(p j) w -> p j w", j=4)
         raws = {}
         for pair in range(2):
-            c0 = 0
-            for i, w in enumerate(LOADS[pair]):
+            for i, (c0, w) in enumerate(LOADS[pair]):
                 raw = keep.tile([P, 2, w], F32, name=f"raw{pair}_{i}")
                 nc.sync.dma_start(out=raw[:], in_=x4[:, 2 * pair : 2 * pair + 2, c0 : c0 + w])
                 raws[pair, i] = (raw, c0, w)
                 if pair == 0 and i == 0:
                     nc.sync.dma_start(offsets[:], offs)
-                c0 = c0 + w
         w14 = w1.rearrange("(p j) c -> p j c", j=4)
         wraw = []
         for half in range(2):
@@ -66,10 +68,8 @@ def tile_picked_modgate_mlpsilu_l_kernel(tc, xT, gate, w1, w2_words, w2_scales, 
         ident = keep.tile([P, P], F32, name="ident")
         make_identity(nc, ident[:])
         window = keep.tile([P, T], F32, name="window")
-        nc.gpsimd.memset(window[:], 0.0)
+        nc.vector.memset(window[:], 0.0)
 
-        shared = keep.tile([P, T + 2 * CH], F32, name="shared", align_bytes=64)
-        gwin = shared[:, 0:T]
         for q in range(4):
             bank = banks.tile([P, 4, P], F32, name="bank")
             for r in range(4):
@@ -80,80 +80,75 @@ def tile_picked_modgate_mlpsilu_l_kernel(tc, xT, gate, w1, w2_words, w2_scales, 
                 in_=bank[:].rearrange("i r p -> i p r"),
             )
         gsel = keep.tile([P, S], F32, name="gsel")
-        for c in range(NCH):
-            nc.vector.tensor_copy(out=gsel[:, c * CH : (c + 1) * CH], in_=gwin.indirect(offsets[:, c * CH // 16 : (c + 1) * CH // 16]))
+        nc.vector.tensor_copy(out=gsel[:], in_=gwin.indirect(offsets[:]))
 
-        xpair = [keep.tile([P, 2 * T], BF16, name=f"xpair{pair}") for pair in range(2)]
-        xg23 = keep.tile([P, 8 * CH], BF16, name="xg23", align_bytes=64)
-        xg = [shared[:, 0 : 2 * CH].bitcast(BF16), shared[:, 2 * CH : 4 * CH].bitcast(BF16), xg23[:, 0 : 4 * CH], xg23[:, 4 * CH : 8 * CH]]
-        g23 = [shared[:, T - 2 * CH : T].bitcast(U32), shared[:, T : T + 2 * CH].bitcast(U32)]
-        g23_both = shared[:, T - 2 * CH : T + 2 * CH].bitcast(U32).rearrange("p (u n) -> p n u", u=2)
+        def entries(c0, c1):
+            return offsets[:, c0 * CH // 16 : c1 * CH // 16]
 
-        def gather23(pair):
-            nc.vector.tensor_copy(out=g23[pair], in_=xpair[pair][:].bitcast(U32).indirect(offsets[:, 2 * CH // 16 : 4 * CH // 16]))
+        xg = keep.tile([P, 6 * CH], F32, name="xg", align_bytes=64)
+        xg3 = keep.tile([P, 2 * CH], F32, name="xg3", align_bytes=64)
+        late = keep.tile([P, CH + 1024], F32, name="late", align_bytes=64)
+        g3 = [late[:, 0:CH].bitcast(U32), late[:, CH : 2 * CH].bitcast(U32)]
+        g3_both = late[:, 0 : 2 * CH].bitcast(U32).rearrange("p (u n) -> p n u", u=2)
+        wgrp = late[:, CH : CH + 1024].bitcast(BF16)
 
         def cast(engine_copy, pair, i, a, b):
             raw, c0, w = raws[pair, i]
             engine_copy(
-                out=xpair[pair][:, 2 * (c0 + a) : 2 * (c0 + b)].rearrange("p (c j) -> p c j", j=2),
+                out=xpair[pair][:, c0 + a : c0 + b].bitcast(BF16).rearrange("p (c j) -> p c j", j=2),
                 in_=raw[:, :, a:b].rearrange("p j c -> p c j"),
             )
 
-        def gather(pair, c):
+        def gather(pair, c0, c1, win):
             nc.vector.tensor_copy(
-                out=xg[c].bitcast(U32).rearrange("p (n u) -> p n u", u=2)[:, :, pair],
-                in_=xpair[pair][:].bitcast(U32).indirect(offsets[:, c * CH // 16 : (c + 1) * CH // 16]),
+                out=xg[:, 2 * CH * c0 : 2 * CH * c1].bitcast(U32).rearrange("p (n u) -> p n u", u=2)[:, :, pair],
+                in_=win.bitcast(U32).indirect(entries(c0, c1)),
             )
 
-        for i, w in enumerate(LOADS[0]):
-            cast(nc.vector.tensor_copy if i == 0 else nc.scalar.copy, 0, i, 0, w)
-        gather(0, 0)
-        gather(0, 1)
-        gather23(0)
-        for i, w in enumerate(LOADS[1]):
-            cast(nc.scalar.copy, 1, i, 0, w)
+        cast(nc.scalar.copy, 0, 0, 0, 1024)
+        cast(nc.vector.tensor_copy, 0, 1, 0, 384)
+        cast(nc.scalar.copy, 0, 1, 384, 1024)
+        nc.vector.tensor_copy(out=g3[0], in_=xpair[0].bitcast(U32).indirect(entries(3, 4)))
 
-        xcodes = [keep.tile([P, CH], U32, name=f"xcodes{c}", align_bytes=64) for c in range(NCH)]
-        xscales = [keep.tile([P, CH], U8, name=f"xscales{c}", align_bytes=64) for c in range(NCH)]
+        gather(0, 0, 3, tables[:, T - SPARE : 2 * T])
+        cast(nc.scalar.copy, 1, 0, 0, 1024)
+        cast(nc.vector.tensor_copy, 1, 1, 0, 640)
+        cast(nc.scalar.copy, 1, 1, 640, 1024)
 
-        def quant_x(c):
-            nc.vector.quantize_mx(out=xcodes[c][:].bitcast(FP8X4), scales=xscales[c][:], in_=xg[c])
-
-        wgrp0 = keep.tile([P, 1024], BF16, name="wgrp0", align_bytes=64)
-        wgrp = [wgrp0[:], shared[:, T : T + 2 * CH].bitcast(BF16)]
+        xc01 = keep.tile([P, 2 * CH], U32, name="xc01", align_bytes=64)
+        xc2 = keep.tile([P, CH], U32, name="xc2", align_bytes=64)
+        xc3 = keep.tile([P, CH], U32, name="xc3", align_bytes=64)
+        xcodes = [xc01[:, 0:CH], xc01[:, CH : 2 * CH], xc2[:], xc3[:]]
+        xsc = keep.tile([P, S], U8, name="xsc", align_bytes=64)
+        xscales = [xsc[:, c * CH : (c + 1) * CH] for c in range(NCH)]
         wcodes = keep.tile([P, H], U32, name="wcodes", align_bytes=64)
         wscales = keep.tile([P, H], U8, name="wscales", align_bytes=64)
 
         def cast_w(half):
             nc.scalar.copy(
-                out=wgrp[half].rearrange("p (t m j) -> p m t j", t=4, j=4),
+                out=wgrp.rearrange("p (t m j) -> p m t j", t=4, j=4)[:, 64 * half : 64 * half + 64],
                 in_=wraw[half][:].rearrange("p j (m t) -> p m t j", t=4),
             )
 
-        def quant_w(half):
-            for t in range(4):
-                cols = slice(128 * t + 64 * half, 128 * t + 64 * half + 64)
-                nc.vector.quantize_mx(out=wcodes[:, cols].bitcast(FP8X4), scales=wscales[:, cols], in_=wgrp[half][:, 256 * t : 256 * t + 256])
-
         cast_w(0)
         cast_w(1)
-        gather(1, 0)
-        gather(1, 1)
-        quant_x(0)
-        quant_w(0)
-        quant_w(1)
-        quant_x(1)
-        gather23(1)
-        nc.vector.tensor_copy(out=xg23[:].bitcast(U32).rearrange("p (n u) -> p n u", u=2), in_=g23_both)
-        quant_x(2)
-        quant_x(3)
+        gather(1, 0, 2, xpair[1])
+        gather(1, 2, 3, xpair[1])
+        nc.vector.quantize_mx(out=xc01[:].bitcast(FP8X4), scales=xsc[:, 0 : 2 * CH], in_=xg[:, 0 : 4 * CH].bitcast(BF16))
+        for u in range(2):
+            cols = slice(256 * u, 256 * u + 256)
+            nc.vector.quantize_mx(out=wcodes[:, cols].bitcast(FP8X4), scales=wscales[:, cols], in_=wgrp[:, 1024 * u : 1024 * u + 1024])
+        nc.vector.tensor_copy(out=g3[1], in_=xpair[1].bitcast(U32).indirect(entries(3, 4)))
+        nc.vector.quantize_mx(out=xcodes[2].bitcast(FP8X4), scales=xscales[2], in_=xg[:, 4 * CH : 6 * CH].bitcast(BF16))
+        nc.vector.tensor_copy(out=xg3[:].bitcast(U32).rearrange("p (n u) -> p n u", u=2), in_=g3_both)
+        nc.vector.quantize_mx(out=xcodes[3].bitcast(FP8X4), scales=xscales[3], in_=xg3[:].bitcast(BF16))
 
-        hb = [keep.tile([P, 4 * CH], BF16, name=f"hb{c}", align_bytes=64) for c in range(NCH)]
-        hcodes = [keep.tile([P, CH], U32, name=f"hcodes{c}", align_bytes=64) for c in range(NCH)]
+        hb, hcodes = {}, {}
         hscales = [keep.tile([P, CH], U8, name=f"hscales{c}", align_bytes=64) for c in range(NCH)]
         ysb = [keep.tile([P, CH], F32, name=f"ysb{c}") for c in range(NCH)]
 
         def layer1(c):
+            hb[c] = keep.tile([P, 4 * CH], BF16, name=f"hb{c}", tag=f"hcodes{c - 2}", align_bytes=64)
             for s in range(CH // P):
                 cols = slice(s * P, (s + 1) * P)
                 bank = banks.tile([P, 4, P], F32, name="bank")
@@ -175,6 +170,7 @@ def tile_picked_modgate_mlpsilu_l_kernel(tc, xT, gate, w1, w2_words, w2_scales, 
                 )
 
         def layer2(c):
+            hcodes[c] = keep.tile([P, CH], U32, name=f"hcodes{c}", tag=f"hcodes{c}", align_bytes=64)
             nc.vector.quantize_mx(out=hcodes[c][:].bitcast(FP8X4), scales=hscales[c][:], in_=hb[c][:])
             yb = ybanks.tile([P, CH], F32, name="yb")
             nc.tensor.matmul_mx(

@@ -85,12 +85,17 @@ def tile_picked_modgate_mlpsilu_l_kernel(tc, xT, gate, w1, w2_words, w2_scales, 
         def entries(c0, c1):
             return offsets[:, c0 * CH // 16 : c1 * CH // 16]
 
-        xg = keep.tile([P, 6 * CH], F32, name="xg", align_bytes=64)
-        xg3 = keep.tile([P, 2 * CH], F32, name="xg3", align_bytes=64)
-        late = keep.tile([P, CH + 1024], F32, name="late", align_bytes=64)
-        g3 = [late[:, 0:CH].bitcast(U32), late[:, CH : 2 * CH].bitcast(U32)]
-        g3_both = late[:, 0 : 2 * CH].bitcast(U32).rearrange("p (u n) -> p n u", u=2)
-        wgrp = late[:, CH : CH + 1024].bitcast(BF16)
+        xg = keep.tile([P, 2 * S], F32, name="xg", align_bytes=64)
+        gab = keep.tile([P, 2 * S], U32, name="gab", align_bytes=64)
+        gab_both = gab[:].rearrange("p (u n) -> p n u", u=2)
+        wgrp_tile = keep.tile([P, 2048], BF16, name="wgrp", align_bytes=64)
+        wgrp = wgrp_tile[:]
+
+        def weave(engine_copy, c):
+            engine_copy(
+                out=xg[:, 2 * CH * c : 2 * CH * (c + 1)].bitcast(U32).rearrange("p (n u) -> p n u", u=2),
+                in_=gab_both[:, CH * c : CH * (c + 1)],
+            )
 
         def cast(engine_copy, pair, i, a, b):
             raw, c0, w = raws[pair, i]
@@ -101,24 +106,22 @@ def tile_picked_modgate_mlpsilu_l_kernel(tc, xT, gate, w1, w2_words, w2_scales, 
 
         def gather(pair, c0, c1, win):
             nc.vector.tensor_copy(
-                out=xg[:, 2 * CH * c0 : 2 * CH * c1].bitcast(U32).rearrange("p (n u) -> p n u", u=2)[:, :, pair],
+                out=gab[:, S * pair + CH * c0 : S * pair + CH * c1],
                 in_=win.bitcast(U32).indirect(entries(c0, c1)),
             )
 
         cast(nc.scalar.copy, 0, 0, 0, 1024)
         cast(nc.vector.tensor_copy, 0, 1, 0, 384)
         cast(nc.scalar.copy, 0, 1, 384, 1024)
-        nc.vector.tensor_copy(out=g3[0], in_=xpair[0].bitcast(U32).indirect(entries(3, 4)))
 
-        gather(0, 0, 3, tables[:, T - SPARE : 2 * T])
+        gather(0, 0, 4, tables[:, T - SPARE : 2 * T])
         cast(nc.scalar.copy, 1, 0, 0, 1024)
         cast(nc.vector.tensor_copy, 1, 1, 0, 640)
         cast(nc.scalar.copy, 1, 1, 640, 1024)
 
         xc01 = keep.tile([P, 2 * CH], U32, name="xc01", align_bytes=64)
-        xc2 = keep.tile([P, CH], U32, name="xc2", align_bytes=64)
-        xc3 = keep.tile([P, CH], U32, name="xc3", align_bytes=64)
-        xcodes = [xc01[:, 0:CH], xc01[:, CH : 2 * CH], xc2[:], xc3[:]]
+        xc23 = keep.tile([P, 2 * CH], U32, name="xc23", align_bytes=64)
+        xcodes = [xc01[:, 0:CH], xc01[:, CH : 2 * CH], xc23[:, 0:CH], xc23[:, CH : 2 * CH]]
         xsc = keep.tile([P, S], U8, name="xsc", align_bytes=64)
         xscales = [xsc[:, c * CH : (c + 1) * CH] for c in range(NCH)]
         wcodes = keep.tile([P, H], U32, name="wcodes", align_bytes=64)
@@ -133,15 +136,17 @@ def tile_picked_modgate_mlpsilu_l_kernel(tc, xT, gate, w1, w2_words, w2_scales, 
         cast_w(0)
         cast_w(1)
         gather(1, 0, 2, xpair[1])
-        gather(1, 2, 3, xpair[1])
-        nc.vector.quantize_mx(out=xc01[:].bitcast(FP8X4), scales=xsc[:, 0 : 2 * CH], in_=xg[:, 0 : 4 * CH].bitcast(BF16))
+        gather(1, 2, 4, xpair[1])
+        weave(nc.vector.tensor_copy, 0)
+        weave(nc.vector.tensor_copy, 1)
+        weave(nc.scalar.copy, 2)
+        weave(nc.scalar.copy, 3)
+        for c in range(2):
+            nc.vector.quantize_mx(out=xcodes[c].bitcast(FP8X4), scales=xscales[c], in_=xg[:, 2 * CH * c : 2 * CH * (c + 1)].bitcast(BF16))
         for u in range(2):
             cols = slice(256 * u, 256 * u + 256)
             nc.vector.quantize_mx(out=wcodes[:, cols].bitcast(FP8X4), scales=wscales[:, cols], in_=wgrp[:, 1024 * u : 1024 * u + 1024])
-        nc.vector.tensor_copy(out=g3[1], in_=xpair[1].bitcast(U32).indirect(entries(3, 4)))
-        nc.vector.quantize_mx(out=xcodes[2].bitcast(FP8X4), scales=xscales[2], in_=xg[:, 4 * CH : 6 * CH].bitcast(BF16))
-        nc.vector.tensor_copy(out=xg3[:].bitcast(U32).rearrange("p (n u) -> p n u", u=2), in_=g3_both)
-        nc.vector.quantize_mx(out=xcodes[3].bitcast(FP8X4), scales=xscales[3], in_=xg3[:].bitcast(BF16))
+        nc.vector.quantize_mx(out=xc23[:].bitcast(FP8X4), scales=xsc[:, 2 * CH : 4 * CH], in_=xg[:, 4 * CH : 8 * CH].bitcast(BF16))
 
         hb, hcodes = {}, {}
         hscales = [keep.tile([P, CH], U8, name=f"hscales{c}", align_bytes=64) for c in range(NCH)]

@@ -5,7 +5,7 @@ from concourse.masks import make_identity
 
 K, T, S, H, N = 512, 2048, 1024, 512, 128
 FLOPS = 2 * K * H * S + 2 * H * N * S
-BYTES = 4 * K * T + 4 * T + 4 * K * H + 128 * 256 + 16 * 128 + 2 * 128 * 64 + 4 * N * T
+BYTES = 4 * K * T + 4 * T + 4 * K * H + H * N // 2 + H * N // 32 + 2 * 128 * (S // 16) + 4 * N * T
 
 F32 = mybir.dt.float32
 BF16 = mybir.dt.bfloat16
@@ -19,190 +19,199 @@ SILU = mybir.ActivationFunctionType.Silu
 MULT = mybir.AluOpType.mult
 
 P = 128
-CH = 256
-NCH = S // CH
-LOADS = [[(1024, 1024), (0, 1024)], [(1024, 1024), (0, 1024)]]
+PACK = 4
+CHUNK = 256
+CHUNKS = S // CHUNK
+HALF_T = T // 2
+HALF_H = H // 2
+VECTOR_COLS = 640
 SPARE = 8
+SCORES_PER_ROW = T // P
+H_BANKS = 3
+Y_BANKS = 2
 
 
 def tile_picked_modgate_mlpsilu_l_kernel(tc, xT, gate, w1, w2_words, w2_scales, offs, out):
     nc = tc.nc
     with ExitStack() as ctx:
         keep = ctx.enter_context(tc.tile_pool(name="keep", bufs=1))
-        banks = ctx.enter_context(tc.psum_pool(name="banks", bufs=3))
-        ybanks = ctx.enter_context(tc.psum_pool(name="ybanks", bufs=2))
+        banks = ctx.enter_context(tc.psum_pool(name="banks", bufs=H_BANKS))
+        ybanks = ctx.enter_context(tc.psum_pool(name="ybanks", bufs=Y_BANKS))
 
         offsets = keep.tile([P, S // 16], U16, name="offsets")
-        gcol = keep.tile([P, 16], F32, name="gcol")
-        nc.sync.dma_start(out=gcol[:], in_=gate[0, :].rearrange("(p b) -> p b", b=16))
+        score_cols = keep.tile([P, SCORES_PER_ROW], F32, name="score_cols")
+        nc.sync.dma_start(out=score_cols[:], in_=gate[0, :].rearrange("(p b) -> p b", b=SCORES_PER_ROW))
 
-        tables = keep.tile([P, 3 * T - SPARE], F32, name="tables")
-        gwin = tables[:, 0:T]
-        xpair = [tables[:, T - SPARE : 2 * T - SPARE], tables[:, 2 * T - SPARE : 3 * T - SPARE]]
+        def entries(c0, c1):
+            return offsets[:, c0 * CHUNK // 16 : c1 * CHUNK // 16]
+
+        tables = keep.tile([P, 3 * T], F32, name="tables")
+        score_table = tables[:, 0:T]
+        pair_table = [tables[:, T : 2 * T], tables[:, 2 * T : 3 * T]]
+        nc.vector.memset(pair_table[0][:, 0:SPARE], 0.0)
         warm = keep.tile([P, 1], F32, name="warm")
-        nc.vector.memset(xpair[1][:, 0:SPARE], 0.0)
-        nc.scalar.activation(warm[:], xpair[1][:, 0:1], SILU)
+        nc.vector.memset(pair_table[1][:, 0:SPARE], 0.0)
+        nc.scalar.activation(warm[:], pair_table[1][:, 0:1], SILU)
 
-        x4 = xT.rearrange("(p j) w -> p j w", j=4)
-        raws = {}
+        x_rows = xT.rearrange("(p j) w -> p j w", j=PACK)
+        x_raw = {}
         for pair in range(2):
-            for i, (c0, w) in enumerate(LOADS[pair]):
-                raw = keep.tile([P, 2, w], F32, name=f"raw{pair}_{i}")
-                nc.sync.dma_start(out=raw[:], in_=x4[:, 2 * pair : 2 * pair + 2, c0 : c0 + w])
-                raws[pair, i] = (raw, c0, w)
-                if pair == 0 and i == 0:
+            for first in (HALF_T, 0):
+                raw = keep.tile([P, 2, HALF_T], F32, name=f"x_raw{pair}_{first}")
+                nc.sync.dma_start(out=raw[:], in_=x_rows[:, 2 * pair : 2 * pair + 2, first : first + HALF_T])
+                x_raw[pair, first] = raw
+                if len(x_raw) == 1:
                     nc.sync.dma_start(offsets[:], offs)
-        w14 = w1.rearrange("(p j) c -> p j c", j=4)
-        wraw = []
+        w1_rows = w1.rearrange("(p j) c -> p j c", j=PACK)
+        w1_raw = []
         for half in range(2):
-            wr = keep.tile([P, 4, 256], F32, name=f"wraw{half}")
-            nc.sync.dma_start(out=wr[:], in_=w14[:, :, 256 * half : 256 * half + 256])
-            wraw.append(wr)
-        w2w = keep.tile([P, 256], U8, name="w2w", align_bytes=64)
-        nc.sync.dma_start(out=w2w[:].bitcast(I32), in_=w2_words[0].bitcast(I32))
-        w2s = keep.tile([P, 128], U8, name="w2s", align_bytes=64)
-        nc.vector.memset(w2s[:].bitcast(I32), 0)
+            raw = keep.tile([P, PACK, HALF_H], F32, name=f"w1_raw{half}")
+            nc.sync.dma_start(out=raw[:], in_=w1_rows[:, :, HALF_H * half : HALF_H * (half + 1)])
+            w1_raw.append(raw)
+        w2_codes = keep.tile([P, 2 * N], U8, name="w2_codes", align_bytes=64)
+        nc.sync.dma_start(out=w2_codes[:].bitcast(I32), in_=w2_words[0].bitcast(I32))
+        w2_scale = keep.tile([P, N], U8, name="w2_scale", align_bytes=64)
+        nc.vector.memset(w2_scale[:].bitcast(I32), 0)
         for q in range(4):
-            nc.sync.dma_start(out=w2s[32 * q : 32 * q + 4, :].bitcast(I32), in_=w2_scales[0, 4 * q : 4 * q + 4, :].bitcast(I32))
+            nc.sync.dma_start(out=w2_scale[32 * q : 32 * q + 4, :].bitcast(I32), in_=w2_scales[0, 4 * q : 4 * q + 4, :].bitcast(I32))
 
         ident = keep.tile([P, P], F32, name="ident")
         make_identity(nc, ident[:])
-        window = keep.tile([P, T], F32, name="window")
-        nc.vector.memset(window[:], 0.0)
+        result = keep.tile([P, T], F32, name="result")
+        nc.vector.memset(result[:], 0.0)
 
-        for q in range(4):
+        for q in range(SCORES_PER_ROW // 4):
             bank = banks.tile([P, 4, P], F32, name="bank")
             for r in range(4):
                 b = 4 * q + r
-                nc.tensor.transpose(bank[:, r, :], gcol[:, b : b + 1].to_broadcast([P, P]), ident[:])
+                nc.tensor.transpose(bank[:, r, :], score_cols[:, b : b + 1].to_broadcast([P, P]), ident[:])
             nc.vector.tensor_copy(
-                out=gwin.rearrange("i (p q r) -> i q p r", q=4, r=4)[:, q],
+                out=score_table.rearrange("i (p q r) -> i q p r", q=SCORES_PER_ROW // 4, r=4)[:, q],
                 in_=bank[:].rearrange("i r p -> i p r"),
             )
-        gsel = keep.tile([P, S], F32, name="gsel")
-        nc.vector.tensor_copy(out=gsel[:], in_=gwin.indirect(offsets[:]))
+        scores01 = keep.tile([P, 2 * CHUNK], F32, name="scores01")
+        nc.vector.tensor_copy(out=scores01[:], in_=tables[:, 0 : T + SPARE].indirect(entries(0, 2)))
 
-        def entries(c0, c1):
-            return offsets[:, c0 * CH // 16 : c1 * CH // 16]
+        x_quads = keep.tile([P, 2 * S], F32, name="x_quads", align_bytes=64)
+        picked = keep.tile([P, 2 * S], U32, name="picked", align_bytes=64)
+        w1_bf16 = keep.tile([P, PACK * H], BF16, name="w1_bf16", align_bytes=64)
 
-        xg = keep.tile([P, 2 * S], F32, name="xg", align_bytes=64)
-        gab = keep.tile([P, 2 * S], U32, name="gab", align_bytes=64)
-        gab_both = gab[:].rearrange("p (u n) -> p n u", u=2)
-        wgrp_tile = keep.tile([P, 2048], BF16, name="wgrp", align_bytes=64)
-        wgrp = wgrp_tile[:]
-
-        def weave(engine_copy, c):
-            engine_copy(
-                out=xg[:, 2 * CH * c : 2 * CH * (c + 1)].bitcast(U32).rearrange("p (n u) -> p n u", u=2),
-                in_=gab_both[:, CH * c : CH * (c + 1)],
+        def cast_x(copy, pair, first, a, b):
+            copy(
+                out=pair_table[pair][:, first + a : first + b].bitcast(BF16).rearrange("p (c j) -> p c j", j=2),
+                in_=x_raw[pair, first][:, :, a:b].rearrange("p j c -> p c j"),
             )
 
-        def cast(engine_copy, pair, i, a, b):
-            raw, c0, w = raws[pair, i]
-            engine_copy(
-                out=xpair[pair][:, c0 + a : c0 + b].bitcast(BF16).rearrange("p (c j) -> p c j", j=2),
-                in_=raw[:, :, a:b].rearrange("p j c -> p c j"),
-            )
+        def cast_pair(pair):
+            cast_x(nc.scalar.copy, pair, HALF_T, 0, HALF_T)
+            cast_x(nc.vector.tensor_copy, pair, 0, 0, VECTOR_COLS)
+            cast_x(nc.scalar.copy, pair, 0, VECTOR_COLS, HALF_T)
 
-        def gather(pair, c0, c1, win):
+        def gather_x(pair, c0, c1, window):
             nc.vector.tensor_copy(
-                out=gab[:, S * pair + CH * c0 : S * pair + CH * c1],
-                in_=win.bitcast(U32).indirect(entries(c0, c1)),
+                out=picked[:, S * pair + CHUNK * c0 : S * pair + CHUNK * c1],
+                in_=window.bitcast(U32).indirect(entries(c0, c1)),
             )
 
-        cast(nc.scalar.copy, 0, 0, 0, 1024)
-        cast(nc.vector.tensor_copy, 0, 1, 0, 384)
-        cast(nc.scalar.copy, 0, 1, 384, 1024)
+        def weave(copy, c):
+            copy(
+                out=x_quads[:, 2 * CHUNK * c : 2 * CHUNK * (c + 1)].bitcast(U32).rearrange("p (n u) -> p n u", u=2),
+                in_=picked[:].rearrange("p (u n) -> p n u", u=2)[:, CHUNK * c : CHUNK * (c + 1)],
+            )
 
-        gather(0, 0, 4, tables[:, T - SPARE : 2 * T])
-        cast(nc.scalar.copy, 1, 0, 0, 1024)
-        cast(nc.vector.tensor_copy, 1, 1, 0, 640)
-        cast(nc.scalar.copy, 1, 1, 640, 1024)
+        cast_pair(0)
+        gather_x(0, 0, CHUNKS, tables[:, T : 2 * T + SPARE])
+        cast_pair(1)
 
-        xc01 = keep.tile([P, 2 * CH], U32, name="xc01", align_bytes=64)
-        xc23 = keep.tile([P, 2 * CH], U32, name="xc23", align_bytes=64)
-        xcodes = [xc01[:, 0:CH], xc01[:, CH : 2 * CH], xc23[:, 0:CH], xc23[:, CH : 2 * CH]]
-        xsc = keep.tile([P, S], U8, name="xsc", align_bytes=64)
-        xscales = [xsc[:, c * CH : (c + 1) * CH] for c in range(NCH)]
-        wcodes = keep.tile([P, H], U32, name="wcodes", align_bytes=64)
-        wscales = keep.tile([P, H], U8, name="wscales", align_bytes=64)
+        x_codes01 = keep.tile([P, 2 * CHUNK], U32, name="x_codes01", align_bytes=64)
+        x_codes23 = keep.tile([P, 2 * CHUNK], U32, name="x_codes23", align_bytes=64)
+        x_codes = [tile[:, CHUNK * u : CHUNK * (u + 1)] for tile in (x_codes01, x_codes23) for u in range(2)]
+        x_scale = keep.tile([P, S], U8, name="x_scale", align_bytes=64)
+        w1_codes = keep.tile([P, H], U32, name="w1_codes", align_bytes=64)
+        w1_scale = keep.tile([P, H], U8, name="w1_scale", align_bytes=64)
 
-        def cast_w(half):
+        for half in range(2):
+            m_half = slice(P // 2 * half, P // 2 * (half + 1))
             nc.scalar.copy(
-                out=wgrp.rearrange("p (t m j) -> p m t j", t=4, j=4)[:, 64 * half : 64 * half + 64],
-                in_=wraw[half][:].rearrange("p j (m t) -> p m t j", t=4),
+                out=w1_bf16[:].rearrange("p (t m j) -> p m t j", t=PACK, j=PACK)[:, m_half],
+                in_=w1_raw[half][:].rearrange("p j (m t) -> p m t j", t=PACK),
             )
 
-        cast_w(0)
-        cast_w(1)
-        gather(1, 0, 2, xpair[1])
-        gather(1, 2, 4, xpair[1])
-        weave(nc.vector.tensor_copy, 0)
-        weave(nc.vector.tensor_copy, 1)
-        weave(nc.scalar.copy, 2)
-        weave(nc.scalar.copy, 3)
+        gather_x(1, 0, 2, pair_table[1])
+        gather_x(1, 2, CHUNKS, pair_table[1])
+        for c in range(CHUNKS):
+            weave(nc.vector.tensor_copy if c < 2 else nc.scalar.copy, c)
         for c in range(2):
-            nc.vector.quantize_mx(out=xcodes[c].bitcast(FP8X4), scales=xscales[c], in_=xg[:, 2 * CH * c : 2 * CH * (c + 1)].bitcast(BF16))
-        for u in range(2):
-            cols = slice(256 * u, 256 * u + 256)
-            nc.vector.quantize_mx(out=wcodes[:, cols].bitcast(FP8X4), scales=wscales[:, cols], in_=wgrp[:, 1024 * u : 1024 * u + 1024])
-        nc.vector.quantize_mx(out=xc23[:].bitcast(FP8X4), scales=xsc[:, 2 * CH : 4 * CH], in_=xg[:, 4 * CH : 8 * CH].bitcast(BF16))
+            nc.vector.quantize_mx(
+                out=x_codes[c].bitcast(FP8X4),
+                scales=x_scale[:, CHUNK * c : CHUNK * (c + 1)],
+                in_=x_quads[:, 2 * CHUNK * c : 2 * CHUNK * (c + 1)].bitcast(BF16),
+            )
+        for half in range(2):
+            cols = slice(HALF_H * half, HALF_H * (half + 1))
+            nc.vector.quantize_mx(
+                out=w1_codes[:, cols].bitcast(FP8X4),
+                scales=w1_scale[:, cols],
+                in_=w1_bf16[:, PACK * HALF_H * half : PACK * HALF_H * (half + 1)],
+            )
+        scores23 = w1_bf16[:, PACK * HALF_H : PACK * H].bitcast(F32)
+        nc.vector.tensor_copy(out=scores23, in_=score_table.indirect(entries(2, CHUNKS)))
+        scores = [part[:, CHUNK * u : CHUNK * (u + 1)] for part in (scores01, scores23) for u in range(2)]
+        nc.vector.quantize_mx(
+            out=x_codes23[:].bitcast(FP8X4),
+            scales=x_scale[:, 2 * CHUNK : S],
+            in_=x_quads[:, 4 * CHUNK : 2 * S].bitcast(BF16),
+        )
 
-        hb, hcodes = {}, {}
-        hscales = [keep.tile([P, CH], U8, name=f"hscales{c}", align_bytes=64) for c in range(NCH)]
-        ysb = [keep.tile([P, CH], F32, name=f"ysb{c}") for c in range(NCH)]
+        h_bf16 = {}
+        h_scale = [keep.tile([P, CHUNK], U8, name=f"h_scale{c}", align_bytes=64) for c in range(CHUNKS)]
+        y = [keep.tile([P, CHUNK], F32, name=f"y{c}") for c in range(CHUNKS)]
 
         def layer1(c):
-            hb[c] = keep.tile([P, 4 * CH], BF16, name=f"hb{c}", tag=f"hcodes{c - 2}", align_bytes=64)
-            for s in range(CH // P):
-                cols = slice(s * P, (s + 1) * P)
-                bank = banks.tile([P, 4, P], F32, name="bank")
-                for t in range(4):
-                    wc = slice(t * P, (t + 1) * P)
+            h_bf16[c] = keep.tile([P, PACK * CHUNK], BF16, name=f"h_bf16_{c}", tag=f"h_slot{c - 2}", align_bytes=64)
+            for s in range(CHUNK // P):
+                bank = banks.tile([P, PACK, P], F32, name="bank")
+                for t in range(PACK):
+                    w_cols = slice(t * P, (t + 1) * P)
                     nc.tensor.matmul_mx(
                         out=bank[:, t, :],
-                        lhsT=wcodes[:, wc].bitcast(FP8X4),
-                        lhsT_scale=wscales[:, wc],
-                        rhs=xcodes[c][:, cols].bitcast(FP8X4),
-                        rhs_scale=xscales[c][:, cols],
+                        lhsT=w1_codes[:, w_cols].bitcast(FP8X4),
+                        lhsT_scale=w1_scale[:, w_cols],
+                        rhs=x_codes[c][:, s * P : (s + 1) * P].bitcast(FP8X4),
+                        rhs_scale=x_scale[:, CHUNK * c + s * P : CHUNK * c + (s + 1) * P],
                         start=True,
                         stop=True,
                     )
                 nc.scalar.activation(
-                    hb[c][:, 4 * P * s : 4 * P * (s + 1)].rearrange("p (n t) -> p n t", t=4),
+                    h_bf16[c][:, PACK * P * s : PACK * P * (s + 1)].rearrange("p (n t) -> p n t", t=PACK),
                     bank[:].rearrange("p t n -> p n t"),
                     SILU,
                 )
 
         def layer2(c):
-            hcodes[c] = keep.tile([P, CH], U32, name=f"hcodes{c}", tag=f"hcodes{c}", align_bytes=64)
-            nc.vector.quantize_mx(out=hcodes[c][:].bitcast(FP8X4), scales=hscales[c][:], in_=hb[c][:])
-            yb = ybanks.tile([P, CH], F32, name="yb")
+            h_codes = keep.tile([P, CHUNK], U32, name=f"h_codes{c}", tag=f"h_slot{c}", align_bytes=64)
+            nc.vector.quantize_mx(out=h_codes[:].bitcast(FP8X4), scales=h_scale[c][:], in_=h_bf16[c][:])
+            y_bank = ybanks.tile([P, CHUNK], F32, name="y_bank")
             nc.tensor.matmul_mx(
-                out=yb[:],
-                lhsT=w2w[:].bitcast(FP4X4),
-                lhsT_scale=w2s[:],
-                rhs=hcodes[c][:].bitcast(FP8X4),
-                rhs_scale=hscales[c][:],
+                out=y_bank[:],
+                lhsT=w2_codes[:].bitcast(FP4X4),
+                lhsT_scale=w2_scale[:],
+                rhs=h_codes[:].bitcast(FP8X4),
+                rhs_scale=h_scale[c][:],
                 start=True,
                 stop=True,
             )
-            nc.scalar.copy(out=ysb[c][:], in_=yb[:])
+            nc.scalar.copy(out=y[c][:], in_=y_bank[:])
 
         def scatter(c):
-            nc.vector.tensor_tensor(
-                window[:].indirect(offsets[:, c * CH // 16 : (c + 1) * CH // 16]),
-                ysb[c][:],
-                gsel[:, c * CH : (c + 1) * CH],
-                MULT,
-            )
+            nc.vector.tensor_tensor(result[:].indirect(entries(c, c + 1)), y[c][:], scores[c], MULT)
 
         layer1(0)
-        for c in range(NCH):
+        for c in range(CHUNKS):
             layer2(c)
-            if c + 1 < NCH:
+            if c + 1 < CHUNKS:
                 layer1(c + 1)
             if c > 0:
                 scatter(c - 1)
-        scatter(NCH - 1)
-        nc.sync.dma_start(out=out, in_=window[:])
+        scatter(CHUNKS - 1)
+        nc.sync.dma_start(out=out, in_=result[:])

@@ -24,9 +24,12 @@ CHUNK = 256
 CHUNKS = S // CHUNK
 HALF_T = T // 2
 HALF_H = H // 2
-VECTOR_COLS = 640
+X_LOADS = ((0, 0, 1024, 512), (0, 1024, 1024, 640), (1, 0, 1024, 0), (1, 1024, 512, 512), (1, 1536, 512, 304))
+RAW_SHIFT = 640
+VECTOR_M = 40
+LAP = 16
+WOVEN = S - CHUNK
 SPARE = 8
-SCORES_PER_ROW = T // P
 H_BANKS = 3
 Y_BANKS = 2
 
@@ -36,37 +39,48 @@ def tile_picked_modgate_mlpsilu_l_kernel(tc, xT, gate, w1, w2_words, w2_scales, 
     with ExitStack() as ctx:
         keep = ctx.enter_context(tc.tile_pool(name="keep", bufs=1))
         banks = ctx.enter_context(tc.psum_pool(name="banks", bufs=H_BANKS))
+        score_banks = ctx.enter_context(tc.psum_pool(name="score_banks", bufs=S // (4 * P)))
         ybanks = ctx.enter_context(tc.psum_pool(name="ybanks", bufs=Y_BANKS))
 
         offsets = keep.tile([P, S // 16], U16, name="offsets")
-        score_cols = keep.tile([P, SCORES_PER_ROW], F32, name="score_cols")
-        nc.sync.dma_start(out=score_cols[:], in_=gate[0, :].rearrange("(p b) -> p b", b=SCORES_PER_ROW))
+        tables = keep.tile([P, 3 * T + HALF_T + RAW_SHIFT], F32, name="tables")
+        score_table = tables[:, 0:T]
+        pair_start = (T, 2 * T + HALF_T)
+        pair_table = [tables[:, start : start + T] for start in pair_start]
+        nc.sync.dma_start(out=score_table[P - 1 : P, :], in_=gate[P - 1 : P, :])
+        nc.sync.dma_start(offsets[:], offs)
+        nc.vector.memset(pair_table[0][:, 0:SPARE], 0.0)
+        warm = keep.tile([P, 1], F32, name="warm")
+        nc.scalar.activation(warm[:], pair_table[0][:, 0:1], SILU)
+        nc.vector.memset(score_table[0 : P - 1, :], 0.0)
 
         def entries(c0, c1):
             return offsets[:, c0 * CHUNK // 16 : c1 * CHUNK // 16]
 
-        tables = keep.tile([P, 3 * T], F32, name="tables")
-        score_table = tables[:, 0:T]
-        pair_table = [tables[:, T : 2 * T], tables[:, 2 * T : 3 * T]]
-        nc.vector.memset(pair_table[0][:, 0:SPARE], 0.0)
-        warm = keep.tile([P, 1], F32, name="warm")
-        nc.vector.memset(pair_table[1][:, 0:SPARE], 0.0)
-        nc.scalar.activation(warm[:], pair_table[1][:, 0:1], SILU)
-
+        arena = keep.tile([P, 2 * S - LAP + 2 * CHUNK], F32, name="arena", align_bytes=64)
+        x_raw_e = keep.tile([P, HALF_T], F32, name="x_raw_e")
+        x_raw_c = keep.tile([P, T], F32, name="x_raw_c")
+        x_raw_d = keep.tile([P, HALF_T], F32, name="x_raw_d")
+        landing = [
+            tables[:, pair_start[0] + HALF_T : pair_start[0] + HALF_T + T],
+            tables[:, pair_start[1] + RAW_SHIFT : pair_start[1] + RAW_SHIFT + T],
+            x_raw_c[:],
+            x_raw_d[:],
+            x_raw_e[:],
+        ]
         x_rows = xT.rearrange("(p j) w -> p j w", j=PACK)
-        x_raw = {}
-        for pair in range(2):
-            for first in (HALF_T, 0):
-                raw = keep.tile([P, 2, HALF_T], F32, name=f"x_raw{pair}_{first}")
-                nc.sync.dma_start(out=raw[:], in_=x_rows[:, 2 * pair : 2 * pair + 2, first : first + HALF_T])
-                x_raw[pair, first] = raw
-                if len(x_raw) == 1:
-                    nc.sync.dma_start(offsets[:], offs)
+        x_raw = []
+        for (pair, first, width, split), words in zip(X_LOADS, landing):
+            raw = words.rearrange("p (j c) -> p j c", j=2)
+            nc.sync.dma_start(out=raw, in_=x_rows[:, 2 * pair : 2 * pair + 2, first : first + width])
+            x_raw.append(raw)
         w1_rows = w1.rearrange("(p j) c -> p j c", j=PACK)
+        w1_raw_a = keep.tile([P, PACK * HALF_H], F32, name="w1_raw_a")
+        late = keep.tile([P, 2 * CHUNK + S], F32, name="late", align_bytes=64)
         w1_raw = []
-        for half in range(2):
-            raw = keep.tile([P, PACK, HALF_H], F32, name=f"w1_raw{half}")
-            nc.sync.dma_start(out=raw[:], in_=w1_rows[:, :, HALF_H * half : HALF_H * (half + 1)])
+        for half, words in enumerate((w1_raw_a[:], late[:, CHUNK : CHUNK + PACK * HALF_H])):
+            raw = words.rearrange("p (j c) -> p j c", j=PACK)
+            nc.sync.dma_start(out=raw, in_=w1_rows[:, :, HALF_H * half : HALF_H * (half + 1)])
             w1_raw.append(raw)
         w2_codes = keep.tile([P, 2 * N], U8, name="w2_codes", align_bytes=64)
         nc.sync.dma_start(out=w2_codes[:].bitcast(I32), in_=w2_words[0].bitcast(I32))
@@ -78,75 +92,93 @@ def tile_picked_modgate_mlpsilu_l_kernel(tc, xT, gate, w1, w2_words, w2_scales, 
         ident = keep.tile([P, P], F32, name="ident")
         make_identity(nc, ident[:])
         result = keep.tile([P, T], F32, name="result")
-        nc.vector.memset(result[:], 0.0)
+        nc.gpsimd.memset(result[:], 0.0)
 
-        for q in range(SCORES_PER_ROW // 4):
+        score_row = keep.tile([P, S], F32, name="score_row")
+        nc.vector.tensor_copy(out=score_row[:], in_=tables[:, 0 : T + SPARE].indirect(entries(0, CHUNKS)))
+
+        score_cols = keep.tile([P, S // P], F32, name="score_cols")
+        scores = late[:, 2 * CHUNK : 2 * CHUNK + S]
+
+        def turn_scores(q):
             bank = banks.tile([P, 4, P], F32, name="bank")
             for r in range(4):
                 b = 4 * q + r
+                nc.tensor.transpose(bank[:, r, :], score_row[:, P * b : P * (b + 1)], ident[:])
+            nc.scalar.copy(out=score_cols[:, 4 * q : 4 * q + 4], in_=bank[:, :, P - 1])
+
+        def spread_scores(q):
+            bank = score_banks.tile([P, 4, P], F32, name="score_bank")
+            for r in range(4):
+                b = 4 * q + r
                 nc.tensor.transpose(bank[:, r, :], score_cols[:, b : b + 1].to_broadcast([P, P]), ident[:])
+            nc.scalar.copy(out=scores[:, 4 * P * q : 4 * P * (q + 1)], in_=bank[:].rearrange("p r n -> p (r n)"))
+
+        x_quads = {0: arena[:, 2 * S - LAP : 2 * S - LAP + 2 * CHUNK], 1: late[:, 0 : 2 * CHUNK]}
+        x_quads23 = keep.tile([P, 4 * CHUNK], F32, name="x_quads23", align_bytes=64)
+        picked = arena[:, 0 : 2 * WOVEN].bitcast(U32)
+        w1_bf16 = arena[:, S : S + PACK * H // 2].bitcast(BF16)
+
+        def cast_x(load):
+            pair, first, width, split = X_LOADS[load]
+            for copy, a, b in ((nc.vector.tensor_copy, 0, split), (nc.scalar.copy, split, width)):
+                if a < b:
+                    copy(
+                        out=pair_table[pair][:, first + a : first + b].bitcast(BF16).rearrange("p (c j) -> p c j", j=2),
+                        in_=x_raw[load][:, :, a:b].rearrange("p j c -> p c j"),
+                    )
+
+        def gather_first(pair):
             nc.vector.tensor_copy(
-                out=score_table.rearrange("i (p q r) -> i q p r", q=SCORES_PER_ROW // 4, r=4)[:, q],
-                in_=bank[:].rearrange("i r p -> i p r"),
-            )
-        scores01 = keep.tile([P, 2 * CHUNK], F32, name="scores01")
-        nc.vector.tensor_copy(out=scores01[:], in_=tables[:, 0 : T + SPARE].indirect(entries(0, 2)))
-
-        x_quads = keep.tile([P, 2 * S], F32, name="x_quads", align_bytes=64)
-        picked = keep.tile([P, 2 * S], U32, name="picked", align_bytes=64)
-        w1_bf16 = keep.tile([P, PACK * H], BF16, name="w1_bf16", align_bytes=64)
-
-        def cast_x(copy, pair, first, a, b):
-            copy(
-                out=pair_table[pair][:, first + a : first + b].bitcast(BF16).rearrange("p (c j) -> p c j", j=2),
-                in_=x_raw[pair, first][:, :, a:b].rearrange("p j c -> p c j"),
+                out=x_quads[0][:].bitcast(U32).rearrange("p (n u) -> p n u", u=2)[:, :, pair],
+                in_=pair_table[pair].bitcast(U32).indirect(entries(0, 1)),
             )
 
-        def cast_pair(pair):
-            cast_x(nc.scalar.copy, pair, HALF_T, 0, HALF_T)
-            cast_x(nc.vector.tensor_copy, pair, 0, 0, VECTOR_COLS)
-            cast_x(nc.scalar.copy, pair, 0, VECTOR_COLS, HALF_T)
-
-        def gather_x(pair, c0, c1, window):
+        def gather_x(pair, c0, c1):
             nc.vector.tensor_copy(
-                out=picked[:, S * pair + CHUNK * c0 : S * pair + CHUNK * c1],
-                in_=window.bitcast(U32).indirect(entries(c0, c1)),
+                out=picked[:, WOVEN * pair + CHUNK * (c0 - 1) : WOVEN * pair + CHUNK * (c1 - 1)],
+                in_=pair_table[pair].bitcast(U32).indirect(entries(c0, c1)),
             )
 
-        def weave(copy, c):
+        def weave(copy, quads, c0, c1):
             copy(
-                out=x_quads[:, 2 * CHUNK * c : 2 * CHUNK * (c + 1)].bitcast(U32).rearrange("p (n u) -> p n u", u=2),
-                in_=picked[:].rearrange("p (u n) -> p n u", u=2)[:, CHUNK * c : CHUNK * (c + 1)],
+                out=quads[:].bitcast(U32).rearrange("p (n u) -> p n u", u=2),
+                in_=picked.rearrange("p (u n) -> p n u", u=2)[:, CHUNK * (c0 - 1) : CHUNK * (c1 - 1)],
             )
 
-        cast_pair(0)
-        gather_x(0, 0, CHUNKS, tables[:, T : 2 * T + SPARE])
-        cast_pair(1)
+        def cast_w1(copy, half, a, b):
+            copy(
+                out=w1_bf16.rearrange("p (t m j) -> p m t j", t=PACK, j=PACK)[:, P // 2 * half + a : P // 2 * half + b],
+                in_=w1_raw[half].rearrange("p j (m t) -> p m t j", t=PACK)[:, a:b],
+            )
 
-        x_codes01 = keep.tile([P, 2 * CHUNK], U32, name="x_codes01", align_bytes=64)
-        x_codes23 = keep.tile([P, 2 * CHUNK], U32, name="x_codes23", align_bytes=64)
-        x_codes = [tile[:, CHUNK * u : CHUNK * (u + 1)] for tile in (x_codes01, x_codes23) for u in range(2)]
-        x_scale = keep.tile([P, S], U8, name="x_scale", align_bytes=64)
+        code_tiles = [keep.tile([P, n * CHUNK], U32, name=f"x_codes{g}", align_bytes=64) for g, n in enumerate((1, 1, 2))]
+        scale_tiles = [keep.tile([P, n * CHUNK], U8, name=f"x_scale{g}", align_bytes=64) for g, n in enumerate((1, 1, 2))]
+        x_codes = [code_tiles[0][:], code_tiles[1][:], code_tiles[2][:, 0:CHUNK], code_tiles[2][:, CHUNK : 2 * CHUNK]]
+        x_scale = [scale_tiles[0][:], scale_tiles[1][:], scale_tiles[2][:, 0:CHUNK], scale_tiles[2][:, CHUNK : 2 * CHUNK]]
         w1_codes = keep.tile([P, H], U32, name="w1_codes", align_bytes=64)
         w1_scale = keep.tile([P, H], U8, name="w1_scale", align_bytes=64)
 
-        for half in range(2):
-            m_half = slice(P // 2 * half, P // 2 * (half + 1))
-            nc.scalar.copy(
-                out=w1_bf16[:].rearrange("p (t m j) -> p m t j", t=PACK, j=PACK)[:, m_half],
-                in_=w1_raw[half][:].rearrange("p j (m t) -> p m t j", t=PACK),
-            )
+        def quantize_x(g, quads):
+            nc.vector.quantize_mx(out=code_tiles[g][:].bitcast(FP8X4), scales=scale_tiles[g][:], in_=quads[:].bitcast(BF16))
 
-        gather_x(1, 0, 2, pair_table[1])
-        gather_x(1, 2, CHUNKS, pair_table[1])
-        for c in range(CHUNKS):
-            weave(nc.vector.tensor_copy if c < 2 else nc.scalar.copy, c)
-        for c in range(2):
-            nc.vector.quantize_mx(
-                out=x_codes[c].bitcast(FP8X4),
-                scales=x_scale[:, CHUNK * c : CHUNK * (c + 1)],
-                in_=x_quads[:, 2 * CHUNK * c : 2 * CHUNK * (c + 1)].bitcast(BF16),
-            )
+        cast_x(0)
+        cast_x(1)
+        for q in range(S // (4 * P)):
+            turn_scores(q)
+        gather_first(0)
+        gather_x(0, 1, CHUNKS)
+        for load in (2, 3, 4):
+            cast_x(load)
+        cast_w1(nc.scalar.copy, 0, 0, P // 2)
+        gather_first(1)
+        gather_x(1, 1, 2)
+        quantize_x(0, x_quads[0])
+        cast_w1(nc.scalar.copy, 1, 0, P // 2 - VECTOR_M)
+        cast_w1(nc.vector.tensor_copy, 1, P // 2 - VECTOR_M, P // 2)
+        weave(nc.scalar.copy, x_quads[1], 1, 2)
+        for q in range(S // (4 * P)):
+            spread_scores(q)
         for half in range(2):
             cols = slice(HALF_H * half, HALF_H * (half + 1))
             nc.vector.quantize_mx(
@@ -154,21 +186,15 @@ def tile_picked_modgate_mlpsilu_l_kernel(tc, xT, gate, w1, w2_words, w2_scales, 
                 scales=w1_scale[:, cols],
                 in_=w1_bf16[:, PACK * HALF_H * half : PACK * HALF_H * (half + 1)],
             )
-        scores23 = w1_bf16[:, PACK * HALF_H : PACK * H].bitcast(F32)
-        nc.vector.tensor_copy(out=scores23, in_=score_table.indirect(entries(2, CHUNKS)))
-        scores = [part[:, CHUNK * u : CHUNK * (u + 1)] for part in (scores01, scores23) for u in range(2)]
-        nc.vector.quantize_mx(
-            out=x_codes23[:].bitcast(FP8X4),
-            scales=x_scale[:, 2 * CHUNK : S],
-            in_=x_quads[:, 4 * CHUNK : 2 * S].bitcast(BF16),
-        )
+        gather_x(1, 2, CHUNKS)
 
         h_bf16 = {}
+        y_bank = {}
         h_scale = [keep.tile([P, CHUNK], U8, name=f"h_scale{c}", align_bytes=64) for c in range(CHUNKS)]
         y = [keep.tile([P, CHUNK], F32, name=f"y{c}") for c in range(CHUNKS)]
 
         def layer1(c):
-            h_bf16[c] = keep.tile([P, PACK * CHUNK], BF16, name=f"h_bf16_{c}", tag=f"h_slot{c - 2}", align_bytes=64)
+            h_bf16[c] = keep.tile([P, PACK * CHUNK], BF16, name=f"h_bf16_{c}", align_bytes=64)
             for s in range(CHUNK // P):
                 bank = banks.tile([P, PACK, P], F32, name="bank")
                 for t in range(PACK):
@@ -178,7 +204,7 @@ def tile_picked_modgate_mlpsilu_l_kernel(tc, xT, gate, w1, w2_words, w2_scales, 
                         lhsT=w1_codes[:, w_cols].bitcast(FP8X4),
                         lhsT_scale=w1_scale[:, w_cols],
                         rhs=x_codes[c][:, s * P : (s + 1) * P].bitcast(FP8X4),
-                        rhs_scale=x_scale[:, CHUNK * c + s * P : CHUNK * c + (s + 1) * P],
+                        rhs_scale=x_scale[c][:, s * P : (s + 1) * P],
                         start=True,
                         stop=True,
                     )
@@ -189,11 +215,11 @@ def tile_picked_modgate_mlpsilu_l_kernel(tc, xT, gate, w1, w2_words, w2_scales, 
                 )
 
         def layer2(c):
-            h_codes = keep.tile([P, CHUNK], U32, name=f"h_codes{c}", tag=f"h_slot{c}", align_bytes=64)
+            h_codes = keep.tile([P, CHUNK], U32, name=f"h_codes{c}", align_bytes=64)
             nc.vector.quantize_mx(out=h_codes[:].bitcast(FP8X4), scales=h_scale[c][:], in_=h_bf16[c][:])
-            y_bank = ybanks.tile([P, CHUNK], F32, name="y_bank")
+            y_bank[c] = ybanks.tile([P, CHUNK], F32, name="y_bank")
             nc.tensor.matmul_mx(
-                out=y_bank[:],
+                out=y_bank[c][:],
                 lhsT=w2_codes[:].bitcast(FP4X4),
                 lhsT_scale=w2_scale[:],
                 rhs=h_codes[:].bitcast(FP8X4),
@@ -201,17 +227,23 @@ def tile_picked_modgate_mlpsilu_l_kernel(tc, xT, gate, w1, w2_words, w2_scales, 
                 start=True,
                 stop=True,
             )
-            nc.scalar.copy(out=y[c][:], in_=y_bank[:])
+
+        def copy_y(c):
+            nc.scalar.copy(out=y[c][:], in_=y_bank[c][:])
 
         def scatter(c):
-            nc.vector.tensor_tensor(result[:].indirect(entries(c, c + 1)), y[c][:], scores[c], MULT)
+            nc.vector.tensor_tensor(result[:].indirect(entries(c, c + 1)), y[c][:], scores[:, CHUNK * c : CHUNK * (c + 1)], MULT)
 
         layer1(0)
-        for c in range(CHUNKS):
+        quantize_x(1, x_quads[1])
+        weave(nc.vector.tensor_copy, x_quads23, 2, CHUNKS)
+        layer2(0)
+        quantize_x(2, x_quads23)
+        for c in range(1, CHUNKS):
+            layer1(c)
+            copy_y(c - 1)
             layer2(c)
-            if c + 1 < CHUNKS:
-                layer1(c + 1)
-            if c > 0:
-                scatter(c - 1)
+            scatter(c - 1)
+        copy_y(CHUNKS - 1)
         scatter(CHUNKS - 1)
         nc.sync.dma_start(out=out, in_=result[:])

@@ -23,13 +23,12 @@ PACK = 4
 CHUNK = 256
 CHUNKS = S // CHUNK
 HALF_T = T // 2
+X_LOADS = ((0, 0, 1024, (0, 256)), (0, 1024, 1024, (384, 1024)), (1, 1024, 1024, (0, 256)), (1, 0, 512, (0, 512)), (1, 512, 512, (0, 336)))
 HALF_H = H // 2
-X_LOADS = ((0, 0, 1024, 512), (0, 1024, 1024, 640), (1, 0, 1024, 0), (1, 1024, 512, 512), (1, 1536, 512, 304))
-RAW_SHIFT = 640
 VECTOR_M = 40
 LAP = 16
-WOVEN = S - CHUNK
 SPARE = 8
+HELD = 1280
 H_BANKS = 3
 Y_BANKS = 2
 
@@ -43,43 +42,43 @@ def tile_picked_modgate_mlpsilu_l_kernel(tc, xT, gate, w1, w2_words, w2_scales, 
         ybanks = ctx.enter_context(tc.psum_pool(name="ybanks", bufs=Y_BANKS))
 
         offsets = keep.tile([P, S // 16], U16, name="offsets")
-        tables = keep.tile([P, 3 * T + HALF_T + RAW_SHIFT], F32, name="tables")
+        tables = keep.tile([P, 3 * T], F32, name="tables", align_bytes=64)
         score_table = tables[:, 0:T]
-        pair_start = (T, 2 * T + HALF_T)
-        pair_table = [tables[:, start : start + T] for start in pair_start]
+        pair_table = [tables[:, T : 2 * T], tables[:, 2 * T : 3 * T]]
         nc.sync.dma_start(out=score_table[P - 1 : P, :], in_=gate[P - 1 : P, :])
         nc.sync.dma_start(offsets[:], offs)
         nc.vector.memset(pair_table[0][:, 0:SPARE], 0.0)
-        warm = keep.tile([P, 1], F32, name="warm")
-        nc.scalar.activation(warm[:], pair_table[0][:, 0:1], SILU)
+        zero = keep.tile([P, 1], F32, name="zero")
+        nc.scalar.activation(zero[:], pair_table[0][:, 0:1], SILU)
+        result = keep.tile([P, T], F32, name="result")
+        nc.scalar.copy(out=result[:], in_=zero[:].to_broadcast([P, T]))
         nc.vector.memset(score_table[0 : P - 1, :], 0.0)
 
         def entries(c0, c1):
             return offsets[:, c0 * CHUNK // 16 : c1 * CHUNK // 16]
 
-        arena = keep.tile([P, 2 * S - LAP + 2 * CHUNK], F32, name="arena", align_bytes=64)
-        x_raw_e = keep.tile([P, HALF_T], F32, name="x_raw_e")
+        x_raw_b = keep.tile([P, T], F32, name="x_raw_b")
         x_raw_c = keep.tile([P, T], F32, name="x_raw_c")
         x_raw_d = keep.tile([P, HALF_T], F32, name="x_raw_d")
-        landing = [
-            tables[:, pair_start[0] + HALF_T : pair_start[0] + HALF_T + T],
-            tables[:, pair_start[1] + RAW_SHIFT : pair_start[1] + RAW_SHIFT + T],
-            x_raw_c[:],
-            x_raw_d[:],
-            x_raw_e[:],
-        ]
+        last = keep.tile([P, HALF_T], F32, name="last", align_bytes=64)
+        landing = [pair_table[1], x_raw_b[:], x_raw_c[:], x_raw_d[:], last[:, 0:HALF_T]]
         x_rows = xT.rearrange("(p j) w -> p j w", j=PACK)
-        x_raw = []
-        for (pair, first, width, split), words in zip(X_LOADS, landing):
-            raw = words.rearrange("p (j c) -> p j c", j=2)
-            nc.sync.dma_start(out=raw, in_=x_rows[:, 2 * pair : 2 * pair + 2, first : first + width])
-            x_raw.append(raw)
+        x_raw = {}
+
+        def load_x(load):
+            pair, first, width, share = X_LOADS[load]
+            x_raw[load] = landing[load][:, 0 : 2 * width].rearrange("p (j c) -> p j c", j=2)
+            nc.sync.dma_start(out=x_raw[load], in_=x_rows[:, 2 * pair : 2 * pair + 2, first : first + width])
+
+        for load in range(len(X_LOADS)):
+            load_x(load)
         w1_rows = w1.rearrange("(p j) c -> p j c", j=PACK)
-        w1_raw_a = keep.tile([P, PACK * HALF_H], F32, name="w1_raw_a")
-        late = keep.tile([P, 2 * CHUNK + S], F32, name="late", align_bytes=64)
+        w1_early = keep.tile([P, PACK * HALF_H], F32, name="w1_early")
+        w1_late = keep.tile([P, PACK * HALF_H], F32, name="w1_late", align_bytes=64)
+        w1_words = [w1_early[:], w1_late[:]]
         w1_raw = []
-        for half, words in enumerate((w1_raw_a[:], late[:, CHUNK : CHUNK + PACK * HALF_H])):
-            raw = words.rearrange("p (j c) -> p j c", j=PACK)
+        for half in range(2):
+            raw = w1_words[half].rearrange("p (j c) -> p j c", j=PACK)
             nc.sync.dma_start(out=raw, in_=w1_rows[:, :, HALF_H * half : HALF_H * (half + 1)])
             w1_raw.append(raw)
         w2_codes = keep.tile([P, 2 * N], U8, name="w2_codes", align_bytes=64)
@@ -91,60 +90,62 @@ def tile_picked_modgate_mlpsilu_l_kernel(tc, xT, gate, w1, w2_words, w2_scales, 
 
         ident = keep.tile([P, P], F32, name="ident")
         make_identity(nc, ident[:])
-        result = keep.tile([P, T], F32, name="result")
-        nc.gpsimd.memset(result[:], 0.0)
 
-        score_row = keep.tile([P, S], F32, name="score_row")
-        nc.vector.tensor_copy(out=score_row[:], in_=tables[:, 0 : T + SPARE].indirect(entries(0, CHUNKS)))
+        score_row = pair_table[0][:, HALF_T:T]
+        nc.vector.tensor_copy(out=score_row[:, 0 : S // 2], in_=score_table.indirect(entries(0, 2)))
+        nc.vector.tensor_copy(out=score_row[:, S // 2 : S], in_=tables[:, 0 : T + SPARE].indirect(entries(2, 4)))
 
-        score_cols = keep.tile([P, S // P], F32, name="score_cols")
-        scores = late[:, 2 * CHUNK : 2 * CHUNK + S]
+        score_cols = [pair_table[1][:, HELD : HELD + 4], pair_table[1][:, HALF_T - 4 : HALF_T]]
+        scores = [keep.tile([P, S // 2], F32, name=f"scores{q}") for q in range(2)]
+        score_bank = {}
 
         def turn_scores(q):
             bank = banks.tile([P, 4, P], F32, name="bank")
             for r in range(4):
                 b = 4 * q + r
                 nc.tensor.transpose(bank[:, r, :], score_row[:, P * b : P * (b + 1)], ident[:])
-            nc.scalar.copy(out=score_cols[:, 4 * q : 4 * q + 4], in_=bank[:, :, P - 1])
+            nc.vector.tensor_copy(out=score_cols[q], in_=bank[:, :, P - 1])
 
         def spread_scores(q):
-            bank = score_banks.tile([P, 4, P], F32, name="score_bank")
+            score_bank[q] = score_banks.tile([P, 4, P], F32, name="score_bank")
             for r in range(4):
-                b = 4 * q + r
-                nc.tensor.transpose(bank[:, r, :], score_cols[:, b : b + 1].to_broadcast([P, P]), ident[:])
-            nc.scalar.copy(out=scores[:, 4 * P * q : 4 * P * (q + 1)], in_=bank[:].rearrange("p r n -> p (r n)"))
+                nc.tensor.transpose(score_bank[q][:, r, :], score_cols[q][:, r : r + 1].to_broadcast([P, P]), ident[:])
 
-        x_quads = {0: arena[:, 2 * S - LAP : 2 * S - LAP + 2 * CHUNK], 1: late[:, 0 : 2 * CHUNK]}
+        def copy_scores(q):
+            nc.scalar.copy(out=scores[q][:], in_=score_bank[q][:].rearrange("p r n -> p (r n)"))
+
+        x_quads0 = keep.tile([P, 2 * CHUNK], F32, name="x_quads0", align_bytes=64)
         x_quads23 = keep.tile([P, 4 * CHUNK], F32, name="x_quads23", align_bytes=64)
-        picked = arena[:, 0 : 2 * WOVEN].bitcast(U32)
-        w1_bf16 = arena[:, S : S + PACK * H // 2].bitcast(BF16)
+        x_quads = [x_quads0[:], w1_words[1][:, 0 : 2 * CHUNK], x_quads23[:]]
+        arena = keep.tile([P, 6 * CHUNK], F32, name="arena")
+        picked = arena[:].bitcast(U32)
+        w1_bf16 = last[:].bitcast(BF16)
 
         def cast_x(load):
-            pair, first, width, split = X_LOADS[load]
-            for copy, a, b in ((nc.vector.tensor_copy, 0, split), (nc.scalar.copy, split, width)):
-                if a < b:
+            pair, first, width, (a, b) = X_LOADS[load]
+            rest = (b, width) if a == 0 else (0, a)
+            for copy, (c0, c1) in ((nc.vector.tensor_copy, (a, b)), (nc.scalar.copy, rest)):
+                if c0 < c1:
                     copy(
-                        out=pair_table[pair][:, first + a : first + b].bitcast(BF16).rearrange("p (c j) -> p c j", j=2),
-                        in_=x_raw[load][:, :, a:b].rearrange("p j c -> p c j"),
+                        out=pair_table[pair][:, first + c0 : first + c1].bitcast(BF16).rearrange("p (c j) -> p c j", j=2),
+                        in_=x_raw[load][:, :, c0:c1].rearrange("p j c -> p c j"),
                     )
 
         def gather_first(pair):
             nc.vector.tensor_copy(
-                out=x_quads[0][:].bitcast(U32).rearrange("p (n u) -> p n u", u=2)[:, :, pair],
+                out=x_quads[0].bitcast(U32).rearrange("p (n u) -> p n u", u=2)[:, :, pair],
                 in_=pair_table[pair].bitcast(U32).indirect(entries(0, 1)),
             )
 
-        def gather_x(pair, c0, c1):
+        def gather_x(window, c0, c1, place):
             nc.vector.tensor_copy(
-                out=picked[:, WOVEN * pair + CHUNK * (c0 - 1) : WOVEN * pair + CHUNK * (c1 - 1)],
-                in_=pair_table[pair].bitcast(U32).indirect(entries(c0, c1)),
+                out=picked[:, CHUNK * place : CHUNK * (place + c1 - c0)],
+                in_=window.bitcast(U32).indirect(entries(c0, c1)),
             )
 
-        def weave(copy, quads, c0, c1):
-            copy(
-                out=quads[:].bitcast(U32).rearrange("p (n u) -> p n u", u=2),
-                in_=picked.rearrange("p (u n) -> p n u", u=2)[:, CHUNK * (c0 - 1) : CHUNK * (c1 - 1)],
-            )
+        def weave(copy, g, first, distance, chunks):
+            words = picked[:, CHUNK * first : CHUNK * (first + 2 * distance)].rearrange("p (u n) -> p n u", u=2)
+            copy(out=x_quads[g].bitcast(U32).rearrange("p (n u) -> p n u", u=2), in_=words[:, 0 : CHUNK * chunks])
 
         def cast_w1(copy, half, a, b):
             copy(
@@ -152,33 +153,39 @@ def tile_picked_modgate_mlpsilu_l_kernel(tc, xT, gate, w1, w2_words, w2_scales, 
                 in_=w1_raw[half].rearrange("p j (m t) -> p m t j", t=PACK)[:, a:b],
             )
 
-        code_tiles = [keep.tile([P, n * CHUNK], U32, name=f"x_codes{g}", align_bytes=64) for g, n in enumerate((1, 1, 2))]
-        scale_tiles = [keep.tile([P, n * CHUNK], U8, name=f"x_scale{g}", align_bytes=64) for g, n in enumerate((1, 1, 2))]
-        x_codes = [code_tiles[0][:], code_tiles[1][:], code_tiles[2][:, 0:CHUNK], code_tiles[2][:, CHUNK : 2 * CHUNK]]
-        x_scale = [scale_tiles[0][:], scale_tiles[1][:], scale_tiles[2][:, 0:CHUNK], scale_tiles[2][:, CHUNK : 2 * CHUNK]]
+        x_codes = {}
+        x_scale = {}
+
+        def quantize_x(g, chunks, tag):
+            codes = keep.tile([P, len(chunks) * CHUNK], U32, name=f"x_codes{g}", tag=tag, align_bytes=64)
+            scale = keep.tile([P, len(chunks) * CHUNK], U8, name=f"x_scale{g}", align_bytes=64)
+            nc.vector.quantize_mx(out=codes[:].bitcast(FP8X4), scales=scale[:], in_=x_quads[g].bitcast(BF16))
+            for i, c in enumerate(chunks):
+                x_codes[c] = codes[:, CHUNK * i : CHUNK * (i + 1)]
+                x_scale[c] = scale[:, CHUNK * i : CHUNK * (i + 1)]
+
         w1_codes = keep.tile([P, H], U32, name="w1_codes", align_bytes=64)
         w1_scale = keep.tile([P, H], U8, name="w1_scale", align_bytes=64)
 
-        def quantize_x(g, quads):
-            nc.vector.quantize_mx(out=code_tiles[g][:].bitcast(FP8X4), scales=scale_tiles[g][:], in_=quads[:].bitcast(BF16))
-
         cast_x(0)
-        cast_x(1)
-        for q in range(S // (4 * P)):
+        for q in range(2):
             turn_scores(q)
+        cast_x(1)
+        for q in range(2):
+            spread_scores(q)
+        copy_scores(0)
+        copy_scores(1)
+        gather_x(tables[:, T : 2 * T + HELD], 1, CHUNKS, 0)
         gather_first(0)
-        gather_x(0, 1, CHUNKS)
         for load in (2, 3, 4):
             cast_x(load)
         cast_w1(nc.scalar.copy, 0, 0, P // 2)
         gather_first(1)
-        gather_x(1, 1, 2)
-        quantize_x(0, x_quads[0])
+        gather_x(pair_table[1], 1, 2, 3)
+        quantize_x(0, (0,), "x_codes0")
         cast_w1(nc.scalar.copy, 1, 0, P // 2 - VECTOR_M)
         cast_w1(nc.vector.tensor_copy, 1, P // 2 - VECTOR_M, P // 2)
-        weave(nc.scalar.copy, x_quads[1], 1, 2)
-        for q in range(S // (4 * P)):
-            spread_scores(q)
+        weave(nc.scalar.copy, 1, 0, 3, 1)
         for half in range(2):
             cols = slice(HALF_H * half, HALF_H * (half + 1))
             nc.vector.quantize_mx(
@@ -186,7 +193,9 @@ def tile_picked_modgate_mlpsilu_l_kernel(tc, xT, gate, w1, w2_words, w2_scales, 
                 scales=w1_scale[:, cols],
                 in_=w1_bf16[:, PACK * HALF_H * half : PACK * HALF_H * (half + 1)],
             )
-        gather_x(1, 2, CHUNKS)
+        quantize_x(1, (1,), "x_codes1")
+        gather_x(pair_table[1], 2, CHUNKS, 3)
+        weave(nc.vector.tensor_copy, 2, 1, 2, 2)
 
         h_bf16 = {}
         y_bank = {}
@@ -194,7 +203,7 @@ def tile_picked_modgate_mlpsilu_l_kernel(tc, xT, gate, w1, w2_words, w2_scales, 
         y = [keep.tile([P, CHUNK], F32, name=f"y{c}") for c in range(CHUNKS)]
 
         def layer1(c):
-            h_bf16[c] = keep.tile([P, PACK * CHUNK], BF16, name=f"h_bf16_{c}", align_bytes=64)
+            h_bf16[c] = keep.tile([P, PACK * CHUNK], BF16, name=f"h_bf16_{c}", tag=f"h_codes{c - 2}", align_bytes=64)
             for s in range(CHUNK // P):
                 bank = banks.tile([P, PACK, P], F32, name="bank")
                 for t in range(PACK):
@@ -215,7 +224,7 @@ def tile_picked_modgate_mlpsilu_l_kernel(tc, xT, gate, w1, w2_words, w2_scales, 
                 )
 
         def layer2(c):
-            h_codes = keep.tile([P, CHUNK], U32, name=f"h_codes{c}", align_bytes=64)
+            h_codes = keep.tile([P, CHUNK], U32, name=f"h_codes{c}", tag=f"h_codes{c}", align_bytes=64)
             nc.vector.quantize_mx(out=h_codes[:].bitcast(FP8X4), scales=h_scale[c][:], in_=h_bf16[c][:])
             y_bank[c] = ybanks.tile([P, CHUNK], F32, name="y_bank")
             nc.tensor.matmul_mx(
@@ -232,13 +241,11 @@ def tile_picked_modgate_mlpsilu_l_kernel(tc, xT, gate, w1, w2_words, w2_scales, 
             nc.scalar.copy(out=y[c][:], in_=y_bank[c][:])
 
         def scatter(c):
-            nc.vector.tensor_tensor(result[:].indirect(entries(c, c + 1)), y[c][:], scores[:, CHUNK * c : CHUNK * (c + 1)], MULT)
+            nc.vector.tensor_tensor(result[:].indirect(entries(c, c + 1)), y[c][:], scores[c // 2][:, CHUNK * (c % 2) : CHUNK * (c % 2 + 1)], MULT)
 
         layer1(0)
-        quantize_x(1, x_quads[1])
-        weave(nc.vector.tensor_copy, x_quads23, 2, CHUNKS)
         layer2(0)
-        quantize_x(2, x_quads23)
+        quantize_x(2, (2, 3), "h_codes-2")
         for c in range(1, CHUNKS):
             layer1(c)
             copy_y(c - 1)

@@ -115,9 +115,9 @@ def tile_picked_modgate_mlpsilu_l_kernel(tc, xT, gate, w1, w2_words, w2_scales, 
             nc.scalar.copy(out=scores[q][:], in_=score_bank[q][:].rearrange("p r n -> p (r n)"))
 
         x_quads0 = keep.tile([P, 2 * CHUNK], F32, name="x_quads0", align_bytes=64)
-        x_quads23 = keep.tile([P, 4 * CHUNK], F32, name="x_quads23", align_bytes=64)
-        x_quads = [x_quads0[:], w1_words[1][:, 0 : 2 * CHUNK], x_quads23[:]]
-        arena = keep.tile([P, 6 * CHUNK], F32, name="arena")
+        x_quads3 = keep.tile([P, 2 * CHUNK], F32, name="x_quads3", align_bytes=64)
+        x_quads = [x_quads0[:], w1_words[1][:, 0 : 2 * CHUNK], w1_words[1][:, 2 * CHUNK : 4 * CHUNK], x_quads3[:]]
+        arena = keep.tile([P, 7 * CHUNK], F32, name="arena")
         picked = arena[:].bitcast(U32)
         w1_bf16 = last[:].bitcast(BF16)
 
@@ -181,11 +181,12 @@ def tile_picked_modgate_mlpsilu_l_kernel(tc, xT, gate, w1, w2_words, w2_scales, 
             cast_x(load)
         cast_w1(nc.scalar.copy, 0, 0, P // 2)
         gather_first(1)
-        gather_x(pair_table[1], 1, 2, 3)
-        quantize_x(0, (0,), "x_codes0")
+        gather_x(pair_table[1], 1, 3, 3)
         cast_w1(nc.scalar.copy, 1, 0, P // 2 - VECTOR_M)
         cast_w1(nc.vector.tensor_copy, 1, P // 2 - VECTOR_M, P // 2)
+        quantize_x(0, (0,), "x_codes0")
         weave(nc.scalar.copy, 1, 0, 3, 1)
+        weave(nc.scalar.copy, 2, 1, 3, 1)
         for half in range(2):
             cols = slice(HALF_H * half, HALF_H * (half + 1))
             nc.vector.quantize_mx(
@@ -194,8 +195,9 @@ def tile_picked_modgate_mlpsilu_l_kernel(tc, xT, gate, w1, w2_words, w2_scales, 
                 in_=w1_bf16[:, PACK * HALF_H * half : PACK * HALF_H * (half + 1)],
             )
         quantize_x(1, (1,), "x_codes1")
-        gather_x(pair_table[1], 2, CHUNKS, 3)
-        weave(nc.vector.tensor_copy, 2, 1, 2, 2)
+        gather_x(pair_table[1], 3, CHUNKS, 3)
+        quantize_x(2, (2,), "x_codes2")
+        weave(nc.vector.tensor_copy, 3, 2, 1, 1)
 
         h_bf16 = {}
         y_bank = {}
@@ -245,7 +247,7 @@ def tile_picked_modgate_mlpsilu_l_kernel(tc, xT, gate, w1, w2_words, w2_scales, 
 
         layer1(0)
         layer2(0)
-        quantize_x(2, (2, 3), "h_codes-2")
+        quantize_x(3, (3,), "h_codes-2")
         for c in range(1, CHUNKS):
             layer1(c)
             copy_y(c - 1)

@@ -25,7 +25,7 @@ CHUNKS = S // CHUNK
 HALF_T = T // 2
 X_LOADS = ((0, 0, 1024, (0, 256)), (0, 1024, 1024, (384, 1024)), (1, 1024, 1024, (0, 256)), (1, 0, 512, (0, 512)), (1, 512, 512, (0, 336)))
 HALF_H = H // 2
-VECTOR_M = 40
+VECTOR_M = 32
 LAP = 16
 SPARE = 8
 HELD = 1280
@@ -225,9 +225,18 @@ def tile_picked_modgate_mlpsilu_l_kernel(tc, xT, gate, w1, w2_words, w2_scales, 
                     SILU,
                 )
 
-        def layer2(c):
+        def layer2(c, parts=1, between=None):
             h_codes = keep.tile([P, CHUNK], U32, name=f"h_codes{c}", tag=f"h_codes{c}", align_bytes=64)
-            nc.vector.quantize_mx(out=h_codes[:].bitcast(FP8X4), scales=h_scale[c][:], in_=h_bf16[c][:])
+            width = CHUNK // parts
+            for part in range(parts):
+                cols = slice(width * part, width * (part + 1))
+                if part and between:
+                    between()
+                nc.vector.quantize_mx(
+                    out=h_codes[:, cols].bitcast(FP8X4),
+                    scales=h_scale[c][:, cols],
+                    in_=h_bf16[c][:, PACK * width * part : PACK * width * (part + 1)],
+                )
             y_bank[c] = ybanks.tile([P, CHUNK], F32, name="y_bank")
             nc.tensor.matmul_mx(
                 out=y_bank[c][:],
@@ -248,7 +257,10 @@ def tile_picked_modgate_mlpsilu_l_kernel(tc, xT, gate, w1, w2_words, w2_scales, 
         layer1(0)
         layer2(0)
         quantize_x(3, (3,), "h_codes-2")
-        for c in range(1, CHUNKS):
+        layer1(1)
+        layer2(1, 2, lambda: nc.vector.tensor_copy(out=y[0][:], in_=y_bank[0][:]))
+        scatter(0)
+        for c in range(2, CHUNKS):
             layer1(c)
             copy_y(c - 1)
             layer2(c)

@@ -17,6 +17,7 @@ FP8X4 = mybir.dt.float8_e4m3fn_x4
 FP4X4 = mybir.dt.float4_e2m1fn_x4
 SILU = mybir.ActivationFunctionType.Silu
 MULT = mybir.AluOpType.mult
+ADD = mybir.AluOpType.add
 
 P = 128
 PACK = 4
@@ -31,6 +32,7 @@ SPARE = 8
 HELD = 1280
 H_BANKS = 3
 Y_BANKS = 2
+PIECES = ((0, 1), (1, 3), (3, 5), (5, 8))
 
 
 def tile_picked_modgate_mlpsilu_l_kernel(tc, xT, gate, w1, w2_words, w2_scales, offs, out):
@@ -96,7 +98,9 @@ def tile_picked_modgate_mlpsilu_l_kernel(tc, xT, gate, w1, w2_words, w2_scales, 
         nc.vector.tensor_copy(out=score_row[:, S // 2 : S], in_=tables[:, 0 : T + SPARE].indirect(entries(2, 4)))
 
         score_cols = [pair_table[1][:, HELD : HELD + 4], pair_table[1][:, HALF_T - 4 : HALF_T]]
-        scores = [keep.tile([P, S // 2], F32, name=f"scores{q}") for q in range(2)]
+        scores = keep.tile([P, S], F32, name="scores")
+        zeros = keep.tile([P, P], F32, name="zeros")
+        nc.vector.memset(zeros[:], 0.0)
         score_bank = {}
 
         def turn_scores(q):
@@ -112,7 +116,7 @@ def tile_picked_modgate_mlpsilu_l_kernel(tc, xT, gate, w1, w2_words, w2_scales, 
                 nc.tensor.transpose(score_bank[q][:, r, :], score_cols[q][:, r : r + 1].to_broadcast([P, P]), ident[:])
 
         def copy_scores(q):
-            nc.scalar.copy(out=scores[q][:], in_=score_bank[q][:].rearrange("p r n -> p (r n)"))
+            nc.scalar.copy(out=scores[:, S // 2 * q : S // 2 * (q + 1)], in_=score_bank[q][:].rearrange("p r n -> p (r n)"))
 
         x_quads0 = keep.tile([P, 2 * CHUNK], F32, name="x_quads0", align_bytes=64)
         x_quads3 = keep.tile([P, 2 * CHUNK], F32, name="x_quads3", align_bytes=64)
@@ -201,12 +205,14 @@ def tile_picked_modgate_mlpsilu_l_kernel(tc, xT, gate, w1, w2_words, w2_scales, 
 
         h_bf16 = {}
         y_bank = {}
-        h_scale = [keep.tile([P, CHUNK], U8, name=f"h_scale{c}", align_bytes=64) for c in range(CHUNKS)]
-        y = [keep.tile([P, CHUNK], F32, name=f"y{c}") for c in range(CHUNKS)]
+        y = {}
+        h_codes = {}
 
         def layer1(c):
-            h_bf16[c] = keep.tile([P, PACK * CHUNK], BF16, name=f"h_bf16_{c}", tag=f"h_codes{c - 2}", align_bytes=64)
-            for s in range(CHUNK // P):
+            b0, b1 = PIECES[c]
+            h_bf16[c] = keep.tile([P, PACK * P * (b1 - b0)], BF16, name=f"h_bf16_{c}", tag=f"h_codes{c - 2}", align_bytes=64)
+            for b in range(b0, b1):
+                chunk, s = divmod(b, CHUNK // P)
                 bank = banks.tile([P, PACK, P], F32, name="bank")
                 for t in range(PACK):
                     w_cols = slice(t * P, (t + 1) * P)
@@ -214,57 +220,61 @@ def tile_picked_modgate_mlpsilu_l_kernel(tc, xT, gate, w1, w2_words, w2_scales, 
                         out=bank[:, t, :],
                         lhsT=w1_codes[:, w_cols].bitcast(FP8X4),
                         lhsT_scale=w1_scale[:, w_cols],
-                        rhs=x_codes[c][:, s * P : (s + 1) * P].bitcast(FP8X4),
-                        rhs_scale=x_scale[c][:, s * P : (s + 1) * P],
+                        rhs=x_codes[chunk][:, s * P : (s + 1) * P].bitcast(FP8X4),
+                        rhs_scale=x_scale[chunk][:, s * P : (s + 1) * P],
                         start=True,
                         stop=True,
                     )
                 nc.scalar.activation(
-                    h_bf16[c][:, PACK * P * s : PACK * P * (s + 1)].rearrange("p (n t) -> p n t", t=PACK),
+                    h_bf16[c][:, PACK * P * (b - b0) : PACK * P * (b - b0 + 1)].rearrange("p (n t) -> p n t", t=PACK),
                     bank[:].rearrange("p t n -> p n t"),
                     SILU,
                 )
 
-        def layer2(c, parts=1, between=None):
-            h_codes = keep.tile([P, CHUNK], U32, name=f"h_codes{c}", tag=f"h_codes{c}", align_bytes=64)
-            width = CHUNK // parts
-            for part in range(parts):
-                cols = slice(width * part, width * (part + 1))
-                if part and between:
-                    between()
+        def layer2(c):
+            width = P * (PIECES[c][1] - PIECES[c][0])
+            h_codes[c] = keep.tile([P, width], U32, name=f"h_codes{c}", tag=f"h_codes{c}", align_bytes=64)
+            h_scale = keep.tile([P, width], U8, name=f"h_scale{c}", align_bytes=64)
+            y_bank[c] = ybanks.tile([P, width], F32, name="y_bank")
+            for first in range(0, width, CHUNK):
+                end = min(first + CHUNK, width)
                 nc.vector.quantize_mx(
-                    out=h_codes[:, cols].bitcast(FP8X4),
-                    scales=h_scale[c][:, cols],
-                    in_=h_bf16[c][:, PACK * width * part : PACK * width * (part + 1)],
+                    out=h_codes[c][:, first:end].bitcast(FP8X4),
+                    scales=h_scale[:, first:end],
+                    in_=h_bf16[c][:, PACK * first : PACK * end],
                 )
-            y_bank[c] = ybanks.tile([P, CHUNK], F32, name="y_bank")
-            nc.tensor.matmul_mx(
-                out=y_bank[c][:],
-                lhsT=w2_codes[:].bitcast(FP4X4),
-                lhsT_scale=w2_scale[:],
-                rhs=h_codes[:].bitcast(FP8X4),
-                rhs_scale=h_scale[c][:],
-                start=True,
-                stop=True,
-            )
+                nc.tensor.matmul_mx(
+                    out=y_bank[c][:, first:end],
+                    lhsT=w2_codes[:].bitcast(FP4X4),
+                    lhsT_scale=w2_scale[:],
+                    rhs=h_codes[c][:, first:end].bitcast(FP8X4),
+                    rhs_scale=h_scale[:, first:end],
+                    start=True,
+                    stop=True,
+                )
+            y[c] = keep.tile([P, width], F32, name=f"y{c}")
+
+        def places(c):
+            return result[:].indirect(offsets[:, PIECES[c][0] * P // 16 : PIECES[c][1] * P // 16])
 
         def copy_y(c):
             nc.scalar.copy(out=y[c][:], in_=y_bank[c][:])
 
         def scatter(c):
-            nc.vector.tensor_tensor(result[:].indirect(entries(c, c + 1)), y[c][:], scores[c // 2][:, CHUNK * (c % 2) : CHUNK * (c % 2 + 1)], MULT)
+            nc.vector.tensor_tensor(places(c), y[c][:], scores[:, P * PIECES[c][0] : P * PIECES[c][1]], MULT)
 
         layer1(0)
         layer2(0)
         quantize_x(3, (3,), "h_codes-2")
+        nc.vector.tensor_tensor(y[0][:], y_bank[0][:], scores[:, 0:P], MULT)
         layer1(1)
-        layer2(1, 2, lambda: nc.vector.tensor_copy(out=y[0][:], in_=y_bank[0][:]))
-        scatter(0)
-        for c in range(2, CHUNKS):
+        layer2(1)
+        nc.vector.tensor_tensor(places(0), y[0][:], zeros[:], ADD)
+        for c in range(2, len(PIECES)):
             layer1(c)
             copy_y(c - 1)
             layer2(c)
             scatter(c - 1)
-        copy_y(CHUNKS - 1)
-        scatter(CHUNKS - 1)
+        copy_y(len(PIECES) - 1)
+        scatter(len(PIECES) - 1)
         nc.sync.dma_start(out=out, in_=result[:])

@@ -31,6 +31,7 @@ LAP = 16
 SPARE = 8
 HELD = 1280
 H_BANKS = 3
+WARM_PASSES = 10
 Y_BANKS = 2
 PIECES = ((0, 1), (1, 3), (3, 5), (5, 8))
 
@@ -172,6 +173,9 @@ def tile_picked_modgate_mlpsilu_l_kernel(tc, xT, gate, w1, w2_words, w2_scales, 
         w1_scale = keep.tile([P, H], U8, name="w1_scale", align_bytes=64)
 
         cast_x(0)
+        warm_codes = keep.tile([P, P], U32, name="warm_codes", align_bytes=64)
+        warm_scale = keep.tile([P, P], U8, name="warm_scale", align_bytes=64)
+        nc.vector.quantize_mx(out=warm_codes[:].bitcast(FP8X4), scales=warm_scale[:], in_=pair_table[0][:, 0 : 2 * P].bitcast(BF16))
         for q in range(2):
             turn_scores(q)
         cast_x(1)
@@ -184,6 +188,18 @@ def tile_picked_modgate_mlpsilu_l_kernel(tc, xT, gate, w1, w2_words, w2_scales, 
         for load in (2, 3, 4):
             cast_x(load)
         cast_w1(nc.scalar.copy, 0, 0, P // 2)
+        warm_bank = score_banks.tile([P, 4, P], F32, name="score_bank")
+        nc.tensor.transpose(warm_bank[:, 0, :], w1_early[:, 0:P], ident[:])
+        for r in range(WARM_PASSES):
+            nc.tensor.matmul_mx(
+                out=warm_bank[:, r % 4, :],
+                lhsT=warm_codes[:].bitcast(FP8X4),
+                lhsT_scale=warm_scale[:],
+                rhs=warm_codes[:].bitcast(FP8X4),
+                rhs_scale=warm_scale[:],
+                start=True,
+                stop=True,
+            )
         gather_first(1)
         gather_x(pair_table[1], 1, 3, 3)
         cast_w1(nc.scalar.copy, 1, 0, P // 2 - VECTOR_M)

@@ -32,6 +32,7 @@ SPARE = 8
 HELD = 1280
 H_BANKS = 3
 WARM_PASSES = 10
+WARM_DELAY = 3
 Y_BANKS = 2
 PIECES = ((0, 1), (1, 3), (3, 5), (5, 8))
 
@@ -189,7 +190,8 @@ def tile_picked_modgate_mlpsilu_l_kernel(tc, xT, gate, w1, w2_words, w2_scales, 
             cast_x(load)
         cast_w1(nc.scalar.copy, 0, 0, P // 2)
         warm_bank = score_banks.tile([P, 4, P], F32, name="score_bank")
-        nc.tensor.transpose(warm_bank[:, 0, :], w1_early[:, 0:P], ident[:])
+        for r in range(WARM_DELAY):
+            nc.tensor.transpose(warm_bank[:, r, :], w1_early[:, r * P : (r + 1) * P], ident[:])
         for r in range(WARM_PASSES):
             nc.tensor.matmul_mx(
                 out=warm_bank[:, r % 4, :],

@@ -32,7 +32,7 @@ SPARE = 8
 HELD = 1280
 H_BANKS = 3
 WARM_PASSES = 10
-WARM_DELAY = 3
+WARM_DELAY = 2
 Y_BANKS = 2
 PIECES = ((0, 1), (1, 3), (3, 5), (5, 8))
 
@@ -155,8 +155,8 @@ def tile_picked_modgate_mlpsilu_l_kernel(tc, xT, gate, w1, w2_words, w2_scales, 
 
         def cast_w1(copy, half, a, b):
             copy(
-                out=w1_bf16.rearrange("p (t m j) -> p m t j", t=PACK, j=PACK)[:, P // 2 * half + a : P // 2 * half + b],
-                in_=w1_raw[half].rearrange("p j (m t) -> p m t j", t=PACK)[:, a:b],
+                out=w1_bf16.rearrange("p (t m j) -> p m j t", t=PACK, j=PACK)[:, P // 2 * half + a : P // 2 * half + b],
+                in_=w1_raw[half].rearrange("p j (m t) -> p m j t", t=PACK)[:, a:b],
             )
 
         x_codes = {}

@@ -26,7 +26,6 @@ CHUNKS = S // CHUNK
 HALF_T = T // 2
 X_LOADS = ((0, 0, 1024, (0, 256)), (0, 1024, 1024, (384, 1024)), (1, 1024, 1024, (0, 256)), (1, 0, 512, (0, 512)), (1, 512, 512, (0, 336)))
 HALF_H = H // 2
-VECTOR_M = 32
 LAP = 16
 SPARE = 8
 HELD = 1280
@@ -153,10 +152,10 @@ def tile_picked_modgate_mlpsilu_l_kernel(tc, xT, gate, w1, w2_words, w2_scales, 
             words = picked[:, CHUNK * first : CHUNK * (first + 2 * distance)].rearrange("p (u n) -> p n u", u=2)
             copy(out=x_quads[g].bitcast(U32).rearrange("p (n u) -> p n u", u=2), in_=words[:, 0 : CHUNK * chunks])
 
-        def cast_w1(copy, half, a, b):
+        def cast_w1(copy, half, t0, t1):
             copy(
-                out=w1_bf16.rearrange("p (t m j) -> p m j t", t=PACK, j=PACK)[:, P // 2 * half + a : P // 2 * half + b],
-                in_=w1_raw[half].rearrange("p j (m t) -> p m j t", t=PACK)[:, a:b],
+                out=w1_bf16.rearrange("p (t m j) -> p m j t", t=PACK, j=PACK)[:, P // 2 * half : P // 2 * (half + 1), :, t0:t1],
+                in_=w1_raw[half].rearrange("p j (m t) -> p m j t", t=PACK)[:, :, :, t0:t1],
             )
 
         x_codes = {}
@@ -188,7 +187,7 @@ def tile_picked_modgate_mlpsilu_l_kernel(tc, xT, gate, w1, w2_words, w2_scales, 
         gather_first(0)
         for load in (2, 3, 4):
             cast_x(load)
-        cast_w1(nc.scalar.copy, 0, 0, P // 2)
+        cast_w1(nc.scalar.copy, 0, 0, PACK)
         warm_bank = score_banks.tile([P, 4, P], F32, name="score_bank")
         for r in range(WARM_DELAY):
             nc.tensor.transpose(warm_bank[:, r, :], w1_early[:, r * P : (r + 1) * P], ident[:])
@@ -204,8 +203,8 @@ def tile_picked_modgate_mlpsilu_l_kernel(tc, xT, gate, w1, w2_words, w2_scales, 
             )
         gather_first(1)
         gather_x(pair_table[1], 1, 3, 3)
-        cast_w1(nc.scalar.copy, 1, 0, P // 2 - VECTOR_M)
-        cast_w1(nc.vector.tensor_copy, 1, P // 2 - VECTOR_M, P // 2)
+        cast_w1(nc.scalar.copy, 1, PACK // 2, PACK)
+        cast_w1(nc.vector.tensor_copy, 1, 0, PACK // 2)
         quantize_x(0, (0,), "x_codes0")
         weave(nc.scalar.copy, 1, 0, 3, 1)
         weave(nc.scalar.copy, 2, 1, 3, 1)

@@ -48,7 +48,7 @@ def tile_picked_modgate_mlpsilu_l_kernel(tc, xT, gate, w1, w2_words, w2_scales, 
         tables = keep.tile([P, 3 * T], F32, name="tables", align_bytes=64)
         score_table = tables[:, 0:T]
         pair_table = [tables[:, T : 2 * T], tables[:, 2 * T : 3 * T]]
-        nc.sync.dma_start(out=score_table[P - 1 : P, :], in_=gate[P - 1 : P, :])
+        nc.scalar.dma_start(out=score_table[P - 1 : P, :], in_=gate[P - 1 : P, :])
         nc.sync.dma_start(offsets[:], offs)
         nc.vector.memset(pair_table[0][:, 0:SPARE], 0.0)
         zero = keep.tile([P, 1], F32, name="zero")
@@ -172,6 +172,15 @@ def tile_picked_modgate_mlpsilu_l_kernel(tc, xT, gate, w1, w2_words, w2_scales, 
         w1_codes = keep.tile([P, H], U32, name="w1_codes", align_bytes=64)
         w1_scale = keep.tile([P, H], U8, name="w1_scale", align_bytes=64)
 
+        def quantize_w1(half, t0, t1):
+            for t in range(t0, t1):
+                first = P * t + P // 2 * half
+                nc.vector.quantize_mx(
+                    out=w1_codes[:, first : first + P // 2].bitcast(FP8X4),
+                    scales=w1_scale[:, first : first + P // 2],
+                    in_=w1_bf16[:, PACK * first : PACK * (first + P // 2)],
+                )
+
         cast_x(0)
         warm_codes = keep.tile([P, P], U32, name="warm_codes", align_bytes=64)
         warm_scale = keep.tile([P, P], U8, name="warm_scale", align_bytes=64)
@@ -187,7 +196,8 @@ def tile_picked_modgate_mlpsilu_l_kernel(tc, xT, gate, w1, w2_words, w2_scales, 
         gather_first(0)
         for load in (2, 3, 4):
             cast_x(load)
-        cast_w1(nc.scalar.copy, 0, 0, PACK)
+        cast_w1(nc.scalar.copy, 0, 0, PACK // 2)
+        cast_w1(nc.scalar.copy, 0, PACK // 2, PACK)
         warm_bank = score_banks.tile([P, 4, P], F32, name="score_bank")
         for r in range(WARM_DELAY):
             nc.tensor.transpose(warm_bank[:, r, :], w1_early[:, r * P : (r + 1) * P], ident[:])
@@ -203,18 +213,14 @@ def tile_picked_modgate_mlpsilu_l_kernel(tc, xT, gate, w1, w2_words, w2_scales, 
             )
         gather_first(1)
         gather_x(pair_table[1], 1, 3, 3)
+        quantize_x(0, (0,), "x_codes0")
+        quantize_w1(0, 0, PACK // 2)
         cast_w1(nc.scalar.copy, 1, PACK // 2, PACK)
         cast_w1(nc.vector.tensor_copy, 1, 0, PACK // 2)
-        quantize_x(0, (0,), "x_codes0")
+        quantize_w1(0, PACK // 2, PACK)
         weave(nc.scalar.copy, 1, 0, 3, 1)
         weave(nc.scalar.copy, 2, 1, 3, 1)
-        for half in range(2):
-            cols = slice(HALF_H * half, HALF_H * (half + 1))
-            nc.vector.quantize_mx(
-                out=w1_codes[:, cols].bitcast(FP8X4),
-                scales=w1_scale[:, cols],
-                in_=w1_bf16[:, PACK * HALF_H * half : PACK * HALF_H * (half + 1)],
-            )
+        quantize_w1(1, 0, PACK)
         quantize_x(1, (1,), "x_codes1")
         gather_x(pair_table[1], 3, CHUNKS, 3)
         quantize_x(2, (2,), "x_codes2")

@@ -30,7 +30,7 @@ LAP = 16
 SPARE = 8
 HELD = 1280
 H_BANKS = 3
-WARM_PASSES = 10
+WARM_PASSES = (512, 512, 256)
 WARM_DELAY = 2
 Y_BANKS = 2
 PIECES = ((0, 1), (1, 3), (3, 5), (5, 8))
@@ -53,7 +53,7 @@ def tile_picked_modgate_mlpsilu_l_kernel(tc, xT, gate, w1, w2_words, w2_scales, 
         nc.vector.memset(pair_table[0][:, 0:SPARE], 0.0)
         zero = keep.tile([P, 1], F32, name="zero")
         nc.scalar.activation(zero[:], pair_table[0][:, 0:1], SILU)
-        result = keep.tile([P, T], F32, name="result")
+        result = keep.tile([P, T], F32, name="result", align_bytes=64)
         nc.scalar.copy(out=result[:], in_=zero[:].to_broadcast([P, T]))
         nc.vector.memset(score_table[0 : P - 1, :], 0.0)
 
@@ -182,9 +182,9 @@ def tile_picked_modgate_mlpsilu_l_kernel(tc, xT, gate, w1, w2_words, w2_scales, 
                 )
 
         cast_x(0)
-        warm_codes = keep.tile([P, P], U32, name="warm_codes", align_bytes=64)
-        warm_scale = keep.tile([P, P], U8, name="warm_scale", align_bytes=64)
-        nc.vector.quantize_mx(out=warm_codes[:].bitcast(FP8X4), scales=warm_scale[:], in_=pair_table[0][:, 0 : 2 * P].bitcast(BF16))
+        warm_codes = keep.tile([P, max(WARM_PASSES)], U32, name="warm_codes", align_bytes=64)
+        warm_scale = keep.tile([P, max(WARM_PASSES)], U8, name="warm_scale", align_bytes=64)
+        nc.vector.quantize_mx(out=warm_codes[:].bitcast(FP8X4), scales=warm_scale[:], in_=result[:, 0 : 2 * max(WARM_PASSES)].bitcast(BF16))
         for q in range(2):
             turn_scores(q)
         cast_x(1)
@@ -201,13 +201,13 @@ def tile_picked_modgate_mlpsilu_l_kernel(tc, xT, gate, w1, w2_words, w2_scales, 
         warm_bank = score_banks.tile([P, 4, P], F32, name="score_bank")
         for r in range(WARM_DELAY):
             nc.tensor.transpose(warm_bank[:, r, :], w1_early[:, r * P : (r + 1) * P], ident[:])
-        for r in range(WARM_PASSES):
+        for width in WARM_PASSES:
             nc.tensor.matmul_mx(
-                out=warm_bank[:, r % 4, :],
-                lhsT=warm_codes[:].bitcast(FP8X4),
-                lhsT_scale=warm_scale[:],
-                rhs=warm_codes[:].bitcast(FP8X4),
-                rhs_scale=warm_scale[:],
+                out=warm_bank[:].rearrange("p r n -> p (r n)")[:, 0:width],
+                lhsT=warm_codes[:, 0:P].bitcast(FP8X4),
+                lhsT_scale=warm_scale[:, 0:P],
+                rhs=warm_codes[:, 0:width].bitcast(FP8X4),
+                rhs_scale=warm_scale[:, 0:width],
                 start=True,
                 stop=True,
             )

@@ -27,6 +27,7 @@ HALF_T = T // 2
 X_LOADS = ((0, 0, 1024, (0, 256)), (0, 1024, 1024, (384, 1024)), (1, 1024, 1024, (0, 256)), (1, 0, 512, (0, 512)), (1, 512, 512, (0, 336)))
 HALF_H = H // 2
 LAP = 16
+LINE = 4
 SPARE = 8
 HELD = 1280
 H_BANKS = 3
@@ -132,8 +133,8 @@ def tile_picked_modgate_mlpsilu_l_kernel(tc, xT, gate, w1, w2_words, w2_scales, 
             for copy, (c0, c1) in ((nc.vector.tensor_copy, (a, b)), (nc.scalar.copy, rest)):
                 if c0 < c1:
                     copy(
-                        out=pair_table[pair][:, first + c0 : first + c1].bitcast(BF16).rearrange("p (c j) -> p c j", j=2),
-                        in_=x_raw[load][:, :, c0:c1].rearrange("p j c -> p c j"),
+                        out=pair_table[pair][:, first + c0 : first + c1].bitcast(BF16).rearrange("p (c i j) -> p c j i", i=LINE, j=2),
+                        in_=x_raw[load][:, :, c0:c1].rearrange("p j (c i) -> p c j i", i=LINE),
                     )
 
         def gather_first(pair):
@@ -249,8 +250,8 @@ def tile_picked_modgate_mlpsilu_l_kernel(tc, xT, gate, w1, w2_words, w2_scales, 
                         stop=True,
                     )
                 nc.scalar.activation(
-                    h_bf16[c][:, PACK * P * (b - b0) : PACK * P * (b - b0 + 1)].rearrange("p (n t) -> p n t", t=PACK),
-                    bank[:].rearrange("p t n -> p n t"),
+                    h_bf16[c][:, PACK * P * (b - b0) : PACK * P * (b - b0 + 1)].rearrange("p (n i t) -> p n t i", i=2, t=PACK),
+                    bank[:].rearrange("p t (n i) -> p n t i", i=2),
                     SILU,
                 )
 

@@ -24,7 +24,7 @@ PACK = 4
 CHUNK = 256
 CHUNKS = S // CHUNK
 HALF_T = T // 2
-X_LOADS = ((0, 0, 1024, (0, 256)), (0, 1024, 1024, (384, 1024)), (1, 1024, 1024, (0, 256)), (1, 0, 512, (0, 512)), (1, 512, 512, (0, 336)))
+X_LOADS = ((0, 0, 1024, (0, 448)), (0, 1024, 1024, (384, 1024)), (1, 1024, 1024, (0, 256)), (1, 0, 512, (0, 512)), (1, 512, 512, (0, 336)))
 HALF_H = H // 2
 LAP = 16
 LINE = 4
@@ -185,7 +185,7 @@ def tile_picked_modgate_mlpsilu_l_kernel(tc, xT, gate, w1, w2_words, w2_scales, 
         cast_x(0)
         warm_codes = keep.tile([P, max(WARM_PASSES)], U32, name="warm_codes", align_bytes=64)
         warm_scale = keep.tile([P, max(WARM_PASSES)], U8, name="warm_scale", align_bytes=64)
-        nc.vector.quantize_mx(out=warm_codes[:].bitcast(FP8X4), scales=warm_scale[:], in_=result[:, 0 : 2 * max(WARM_PASSES)].bitcast(BF16))
+        nc.vector.quantize_mx(out=warm_codes[:].bitcast(FP8X4), scales=warm_scale[:], in_=pair_table[0][:, 0 : 2 * max(WARM_PASSES)].bitcast(BF16))
         for q in range(2):
             turn_scores(q)
         cast_x(1)

@@ -77,7 +77,7 @@ def tile_picked_modgate_mlpsilu_l_kernel(tc, xT, gate, w1, w2_words, w2_scales, 
         for load in range(len(X_LOADS)):
             load_x(load)
         w1_rows = w1.rearrange("(p j) c -> p j c", j=PACK)
-        w1_early = keep.tile([P, PACK * HALF_H], F32, name="w1_early")
+        w1_early = keep.tile([P, PACK * HALF_H], F32, name="w1_early", align_bytes=64)
         w1_late = keep.tile([P, PACK * HALF_H], F32, name="w1_late", align_bytes=64)
         w1_words = [w1_early[:], w1_late[:]]
         w1_raw = []
@@ -173,14 +173,12 @@ def tile_picked_modgate_mlpsilu_l_kernel(tc, xT, gate, w1, w2_words, w2_scales, 
         w1_codes = keep.tile([P, H], U32, name="w1_codes", align_bytes=64)
         w1_scale = keep.tile([P, H], U8, name="w1_scale", align_bytes=64)
 
-        def quantize_w1(half, t0, t1):
-            for t in range(t0, t1):
-                first = P * t + P // 2 * half
-                nc.vector.quantize_mx(
-                    out=w1_codes[:, first : first + P // 2].bitcast(FP8X4),
-                    scales=w1_scale[:, first : first + P // 2],
-                    in_=w1_bf16[:, PACK * first : PACK * (first + P // 2)],
-                )
+        def quantize_w1(t0, t1):
+            nc.vector.quantize_mx(
+                out=w1_codes[:, P * t0 : P * t1].bitcast(FP8X4),
+                scales=w1_scale[:, P * t0 : P * t1],
+                in_=w1_bf16[:, PACK * P * t0 : PACK * P * t1],
+            )
 
         cast_x(0)
         warm_codes = keep.tile([P, max(WARM_PASSES)], U32, name="warm_codes", align_bytes=64)
@@ -214,14 +212,13 @@ def tile_picked_modgate_mlpsilu_l_kernel(tc, xT, gate, w1, w2_words, w2_scales, 
             )
         gather_first(1)
         gather_x(pair_table[1], 1, 3, 3)
-        quantize_x(0, (0,), "x_codes0")
-        quantize_w1(0, 0, PACK // 2)
         cast_w1(nc.scalar.copy, 1, PACK // 2, PACK)
         cast_w1(nc.vector.tensor_copy, 1, 0, PACK // 2)
-        quantize_w1(0, PACK // 2, PACK)
+        quantize_x(0, (0,), "w1_early")
+        quantize_w1(0, PACK // 2)
         weave(nc.scalar.copy, 1, 0, 3, 1)
         weave(nc.scalar.copy, 2, 1, 3, 1)
-        quantize_w1(1, 0, PACK)
+        quantize_w1(PACK // 2, PACK)
         quantize_x(1, (1,), "x_codes1")
         gather_x(pair_table[1], 3, CHUNKS, 3)
         quantize_x(2, (2,), "x_codes2")

@@ -24,12 +24,21 @@ PACK = 4
 CHUNK = 256
 CHUNKS = S // CHUNK
 HALF_T = T // 2
-X_LOADS = ((0, 0, 1024, (0, 448)), (0, 1024, 1024, (384, 1024)), (1, 1024, 1024, (0, 256)), (1, 0, 512, (0, 512)), (1, 512, 512, (0, 336)))
+X_LOADS = (
+    (0, 0, 1024, (0, 448)),
+    (0, 1024, 1024, (384, 1024)),
+    (1, 1024, 1024, (0, 400)),
+    (1, 0, 512, (0, 512)),
+    (1, 512, 512, (0, 336)),
+)
 HALF_H = H // 2
-LAP = 16
 LINE = 4
 SPARE = 8
-HELD = 1280
+TURNED = 1280
+HELD = 1424
+PAIR1_PLACE = CHUNKS - 1
+PLACES = 1 + 2 * PAIR1_PLACE
+BANK_BLOCKS = 4
 H_BANKS = 3
 WARM_PASSES = (512, 512, 256)
 WARM_DELAY = 2
@@ -42,7 +51,7 @@ def tile_picked_modgate_mlpsilu_l_kernel(tc, xT, gate, w1, w2_words, w2_scales, 
     with ExitStack() as ctx:
         keep = ctx.enter_context(tc.tile_pool(name="keep", bufs=1))
         banks = ctx.enter_context(tc.psum_pool(name="banks", bufs=H_BANKS))
-        score_banks = ctx.enter_context(tc.psum_pool(name="score_banks", bufs=S // (4 * P)))
+        score_banks = ctx.enter_context(tc.psum_pool(name="score_banks", bufs=S // (BANK_BLOCKS * P)))
         ybanks = ctx.enter_context(tc.psum_pool(name="ybanks", bufs=Y_BANKS))
 
         offsets = keep.tile([P, S // 16], U16, name="offsets")
@@ -70,7 +79,7 @@ def tile_picked_modgate_mlpsilu_l_kernel(tc, xT, gate, w1, w2_words, w2_scales, 
         x_raw = {}
 
         def load_x(load):
-            pair, first, width, share = X_LOADS[load]
+            pair, first, width = X_LOADS[load][0:3]
             x_raw[load] = landing[load][:, 0 : 2 * width].rearrange("p (j c) -> p j c", j=2)
             nc.sync.dma_start(out=x_raw[load], in_=x_rows[:, 2 * pair : 2 * pair + 2, first : first + width])
 
@@ -89,8 +98,9 @@ def tile_picked_modgate_mlpsilu_l_kernel(tc, xT, gate, w1, w2_words, w2_scales, 
         nc.sync.dma_start(out=w2_codes[:].bitcast(I32), in_=w2_words[0].bitcast(I32))
         w2_scale = keep.tile([P, N], U8, name="w2_scale", align_bytes=64)
         nc.vector.memset(w2_scale[:].bitcast(I32), 0)
-        for q in range(4):
-            nc.sync.dma_start(out=w2_scale[32 * q : 32 * q + 4, :].bitcast(I32), in_=w2_scales[0, 4 * q : 4 * q + 4, :].bitcast(I32))
+        for quadrant in range(4):
+            rows = w2_scales[0, 4 * quadrant : 4 * quadrant + 4, :]
+            nc.sync.dma_start(out=w2_scale[32 * quadrant : 32 * quadrant + 4, :].bitcast(I32), in_=rows.bitcast(I32))
 
         ident = keep.tile([P, P], F32, name="ident")
         make_identity(nc, ident[:])
@@ -99,22 +109,22 @@ def tile_picked_modgate_mlpsilu_l_kernel(tc, xT, gate, w1, w2_words, w2_scales, 
         nc.vector.tensor_copy(out=score_row[:, 0 : S // 2], in_=score_table.indirect(entries(0, 2)))
         nc.vector.tensor_copy(out=score_row[:, S // 2 : S], in_=tables[:, 0 : T + SPARE].indirect(entries(2, 4)))
 
-        score_cols = [pair_table[1][:, HELD : HELD + 4], pair_table[1][:, HALF_T - 4 : HALF_T]]
+        score_cols = [pair_table[1][:, TURNED : TURNED + BANK_BLOCKS], pair_table[1][:, HALF_T - BANK_BLOCKS : HALF_T]]
         scores = keep.tile([P, S], F32, name="scores")
         zeros = keep.tile([P, P], F32, name="zeros")
         nc.vector.memset(zeros[:], 0.0)
         score_bank = {}
 
         def turn_scores(q):
-            bank = banks.tile([P, 4, P], F32, name="bank")
-            for r in range(4):
-                b = 4 * q + r
+            bank = banks.tile([P, BANK_BLOCKS, P], F32, name="bank")
+            for r in range(BANK_BLOCKS):
+                b = BANK_BLOCKS * q + r
                 nc.tensor.transpose(bank[:, r, :], score_row[:, P * b : P * (b + 1)], ident[:])
             nc.vector.tensor_copy(out=score_cols[q], in_=bank[:, :, P - 1])
 
         def spread_scores(q):
-            score_bank[q] = score_banks.tile([P, 4, P], F32, name="score_bank")
-            for r in range(4):
+            score_bank[q] = score_banks.tile([P, BANK_BLOCKS, P], F32, name="score_bank")
+            for r in range(BANK_BLOCKS):
                 nc.tensor.transpose(score_bank[q][:, r, :], score_cols[q][:, r : r + 1].to_broadcast([P, P]), ident[:])
 
         def copy_scores(q):
@@ -123,7 +133,7 @@ def tile_picked_modgate_mlpsilu_l_kernel(tc, xT, gate, w1, w2_words, w2_scales, 
         x_quads0 = keep.tile([P, 2 * CHUNK], F32, name="x_quads0", align_bytes=64)
         x_quads3 = keep.tile([P, 2 * CHUNK], F32, name="x_quads3", align_bytes=64)
         x_quads = [x_quads0[:], w1_words[1][:, 0 : 2 * CHUNK], w1_words[1][:, 2 * CHUNK : 4 * CHUNK], x_quads3[:]]
-        arena = keep.tile([P, 7 * CHUNK], F32, name="arena")
+        arena = keep.tile([P, PLACES * CHUNK], F32, name="arena")
         picked = arena[:].bitcast(U32)
         w1_bf16 = last[:].bitcast(BF16)
 
@@ -149,9 +159,10 @@ def tile_picked_modgate_mlpsilu_l_kernel(tc, xT, gate, w1, w2_words, w2_scales, 
                 in_=window.bitcast(U32).indirect(entries(c0, c1)),
             )
 
-        def weave(copy, g, first, distance, chunks):
-            words = picked[:, CHUNK * first : CHUNK * (first + 2 * distance)].rearrange("p (u n) -> p n u", u=2)
-            copy(out=x_quads[g].bitcast(U32).rearrange("p (n u) -> p n u", u=2), in_=words[:, 0 : CHUNK * chunks])
+        def weave(copy, chunk, place):
+            first = chunk - 1
+            words = picked[:, CHUNK * first : CHUNK * (2 * place - first)].rearrange("p (u n) -> p n u", u=2)
+            copy(out=x_quads[chunk].bitcast(U32).rearrange("p (n u) -> p n u", u=2), in_=words[:, 0:CHUNK])
 
         def cast_w1(copy, half, t0, t1):
             copy(
@@ -162,13 +173,12 @@ def tile_picked_modgate_mlpsilu_l_kernel(tc, xT, gate, w1, w2_words, w2_scales, 
         x_codes = {}
         x_scale = {}
 
-        def quantize_x(g, chunks, tag):
-            codes = keep.tile([P, len(chunks) * CHUNK], U32, name=f"x_codes{g}", tag=tag, align_bytes=64)
-            scale = keep.tile([P, len(chunks) * CHUNK], U8, name=f"x_scale{g}", align_bytes=64)
-            nc.vector.quantize_mx(out=codes[:].bitcast(FP8X4), scales=scale[:], in_=x_quads[g].bitcast(BF16))
-            for i, c in enumerate(chunks):
-                x_codes[c] = codes[:, CHUNK * i : CHUNK * (i + 1)]
-                x_scale[c] = scale[:, CHUNK * i : CHUNK * (i + 1)]
+        def quantize_x(chunk, tag):
+            codes = keep.tile([P, CHUNK], U32, name=f"x_codes{chunk}", tag=tag, align_bytes=64)
+            scale = keep.tile([P, CHUNK], U8, name=f"x_scale{chunk}", align_bytes=64)
+            nc.vector.quantize_mx(out=codes[:].bitcast(FP8X4), scales=scale[:], in_=x_quads[chunk].bitcast(BF16))
+            x_codes[chunk] = codes[:, 0:CHUNK]
+            x_scale[chunk] = scale[:, 0:CHUNK]
 
         w1_codes = keep.tile([P, H], U32, name="w1_codes", align_bytes=64)
         w1_scale = keep.tile([P, H], U8, name="w1_scale", align_bytes=64)
@@ -189,15 +199,15 @@ def tile_picked_modgate_mlpsilu_l_kernel(tc, xT, gate, w1, w2_words, w2_scales, 
         cast_x(1)
         for q in range(2):
             spread_scores(q)
-        copy_scores(0)
-        copy_scores(1)
+        for q in range(2):
+            copy_scores(q)
         gather_x(tables[:, T : 2 * T + HELD], 1, CHUNKS, 0)
         gather_first(0)
         for load in (2, 3, 4):
             cast_x(load)
         cast_w1(nc.scalar.copy, 0, 0, PACK // 2)
         cast_w1(nc.scalar.copy, 0, PACK // 2, PACK)
-        warm_bank = score_banks.tile([P, 4, P], F32, name="score_bank")
+        warm_bank = score_banks.tile([P, BANK_BLOCKS, P], F32, name="score_bank")
         for r in range(WARM_DELAY):
             nc.tensor.transpose(warm_bank[:, r, :], w1_early[:, r * P : (r + 1) * P], ident[:])
         for width in WARM_PASSES:
@@ -211,23 +221,22 @@ def tile_picked_modgate_mlpsilu_l_kernel(tc, xT, gate, w1, w2_words, w2_scales, 
                 stop=True,
             )
         gather_first(1)
-        gather_x(pair_table[1], 1, 3, 3)
+        gather_x(pair_table[1], 1, CHUNKS - 1, PAIR1_PLACE)
         cast_w1(nc.scalar.copy, 1, PACK // 2, PACK)
         cast_w1(nc.vector.tensor_copy, 1, 0, PACK // 2)
-        quantize_x(0, (0,), "w1_early")
+        quantize_x(0, "w1_early")
         quantize_w1(0, PACK // 2)
-        weave(nc.scalar.copy, 1, 0, 3, 1)
-        weave(nc.scalar.copy, 2, 1, 3, 1)
+        weave(nc.scalar.copy, 1, PAIR1_PLACE)
+        weave(nc.scalar.copy, 2, PAIR1_PLACE + 1)
         quantize_w1(PACK // 2, PACK)
-        quantize_x(1, (1,), "x_codes1")
-        gather_x(pair_table[1], 3, CHUNKS, 3)
-        quantize_x(2, (2,), "x_codes2")
-        weave(nc.vector.tensor_copy, 3, 2, 1, 1)
+        quantize_x(1, "x_codes1")
+        gather_x(pair_table[1], CHUNKS - 1, CHUNKS, PAIR1_PLACE)
+        quantize_x(2, "x_codes2")
+        weave(nc.vector.tensor_copy, CHUNKS - 1, PAIR1_PLACE)
 
         h_bf16 = {}
         y_bank = {}
         y = {}
-        h_codes = {}
 
         def layer1(c):
             b0, b1 = PIECES[c]
@@ -254,13 +263,13 @@ def tile_picked_modgate_mlpsilu_l_kernel(tc, xT, gate, w1, w2_words, w2_scales, 
 
         def layer2(c):
             width = P * (PIECES[c][1] - PIECES[c][0])
-            h_codes[c] = keep.tile([P, width], U32, name=f"h_codes{c}", tag=f"h_codes{c}", align_bytes=64)
+            h_codes = keep.tile([P, width], U32, name=f"h_codes{c}", tag=f"h_codes{c}", align_bytes=64)
             h_scale = keep.tile([P, width], U8, name=f"h_scale{c}", align_bytes=64)
             y_bank[c] = ybanks.tile([P, width], F32, name="y_bank")
             for first in range(0, width, CHUNK):
                 end = min(first + CHUNK, width)
                 nc.vector.quantize_mx(
-                    out=h_codes[c][:, first:end].bitcast(FP8X4),
+                    out=h_codes[:, first:end].bitcast(FP8X4),
                     scales=h_scale[:, first:end],
                     in_=h_bf16[c][:, PACK * first : PACK * end],
                 )
@@ -268,7 +277,7 @@ def tile_picked_modgate_mlpsilu_l_kernel(tc, xT, gate, w1, w2_words, w2_scales, 
                     out=y_bank[c][:, first:end],
                     lhsT=w2_codes[:].bitcast(FP4X4),
                     lhsT_scale=w2_scale[:],
-                    rhs=h_codes[c][:, first:end].bitcast(FP8X4),
+                    rhs=h_codes[:, first:end].bitcast(FP8X4),
                     rhs_scale=h_scale[:, first:end],
                     start=True,
                     stop=True,
@@ -286,7 +295,7 @@ def tile_picked_modgate_mlpsilu_l_kernel(tc, xT, gate, w1, w2_words, w2_scales, 
 
         layer1(0)
         layer2(0)
-        quantize_x(3, (3,), "h_codes-2")
+        quantize_x(CHUNKS - 1, "h_codes-2")
         nc.vector.tensor_tensor(y[0][:], y_bank[0][:], scores[:, 0:P], MULT)
         layer1(1)
         layer2(1)

from contextlib import ExitStack

import concourse.mybir as mybir
from concourse.masks import make_identity

K, T, S, H, N = 512, 2048, 1024, 512, 128
FLOPS = 2 * K * H * S + 2 * H * N * S
BYTES = 4 * K * T + 4 * T + 4 * K * H + H * N // 2 + H * N // 32 + 2 * 128 * (S // 16) + 4 * N * T

F32 = mybir.dt.float32
BF16 = mybir.dt.bfloat16
U32 = mybir.dt.uint32
I32 = mybir.dt.int32
U16 = mybir.dt.uint16
U8 = mybir.dt.uint8
FP8X4 = mybir.dt.float8_e4m3fn_x4
FP4X4 = mybir.dt.float4_e2m1fn_x4
SILU = mybir.ActivationFunctionType.Silu
MULT = mybir.AluOpType.mult
ADD = mybir.AluOpType.add

P = 128
PACK = 4
CHUNK = 256
CHUNKS = S // CHUNK
HALF_T = T // 2
X_LOADS = (
    (0, 0, 1024, (0, 448)),
    (0, 1024, 1024, (384, 1024)),
    (1, 1024, 1024, (0, 400)),
    (1, 0, 512, (0, 512)),
    (1, 512, 512, (0, 336)),
)
HALF_H = H // 2
LINE = 4
SPARE = 8
TURNED = 1280
HELD = 1424
PAIR1_PLACE = CHUNKS - 1
PLACES = 1 + 2 * PAIR1_PLACE
BANK_BLOCKS = 4
H_BANKS = 3
WARM_PASSES = (512, 512, 256)
WARM_DELAY = 2
Y_BANKS = 2
PIECES = ((0, 1), (1, 3), (3, 5), (5, 8))


def tile_picked_modgate_mlpsilu_l_kernel(tc, xT, gate, w1, w2_words, w2_scales, offs, out):
    nc = tc.nc
    with ExitStack() as ctx:
        keep = ctx.enter_context(tc.tile_pool(name="keep", bufs=1))
        banks = ctx.enter_context(tc.psum_pool(name="banks", bufs=H_BANKS))
        score_banks = ctx.enter_context(tc.psum_pool(name="score_banks", bufs=S // (BANK_BLOCKS * P)))
        ybanks = ctx.enter_context(tc.psum_pool(name="ybanks", bufs=Y_BANKS))

        offsets = keep.tile([P, S // 16], U16, name="offsets")
        tables = keep.tile([P, 3 * T], F32, name="tables", align_bytes=64)
        score_table = tables[:, 0:T]
        pair_table = [tables[:, T : 2 * T], tables[:, 2 * T : 3 * T]]
        nc.scalar.dma_start(out=score_table[P - 1 : P, :], in_=gate[P - 1 : P, :])
        nc.sync.dma_start(offsets[:], offs)
        nc.vector.memset(pair_table[0][:, 0:SPARE], 0.0)
        zero = keep.tile([P, 1], F32, name="zero")
        nc.scalar.activation(zero[:], pair_table[0][:, 0:1], SILU)
        result = keep.tile([P, T], F32, name="result", align_bytes=64)
        nc.scalar.copy(out=result[:], in_=zero[:].to_broadcast([P, T]))
        nc.vector.memset(score_table[0 : P - 1, :], 0.0)

        def entries(c0, c1):
            return offsets[:, c0 * CHUNK // 16 : c1 * CHUNK // 16]

        x_raw_b = keep.tile([P, T], F32, name="x_raw_b")
        x_raw_c = keep.tile([P, T], F32, name="x_raw_c")
        x_raw_d = keep.tile([P, HALF_T], F32, name="x_raw_d")
        last = keep.tile([P, HALF_T], F32, name="last", align_bytes=64)
        landing = [pair_table[1], x_raw_b[:], x_raw_c[:], x_raw_d[:], last[:, 0:HALF_T]]
        x_rows = xT.rearrange("(p j) w -> p j w", j=PACK)
        x_raw = {}

        def load_x(load):
            pair, first, width = X_LOADS[load][0:3]
            x_raw[load] = landing[load][:, 0 : 2 * width].rearrange("p (j c) -> p j c", j=2)
            nc.sync.dma_start(out=x_raw[load], in_=x_rows[:, 2 * pair : 2 * pair + 2, first : first + width])

        for load in range(len(X_LOADS)):
            load_x(load)
        w1_rows = w1.rearrange("(p j) c -> p j c", j=PACK)
        w1_early = keep.tile([P, PACK * HALF_H], F32, name="w1_early", align_bytes=64)
        w1_late = keep.tile([P, PACK * HALF_H], F32, name="w1_late", align_bytes=64)
        w1_words = [w1_early[:], w1_late[:]]
        w1_raw = []
        for half in range(2):
            raw = w1_words[half].rearrange("p (j c) -> p j c", j=PACK)
            nc.sync.dma_start(out=raw, in_=w1_rows[:, :, HALF_H * half : HALF_H * (half + 1)])
            w1_raw.append(raw)
        w2_codes = keep.tile([P, 2 * N], U8, name="w2_codes", align_bytes=64)
        nc.sync.dma_start(out=w2_codes[:].bitcast(I32), in_=w2_words[0].bitcast(I32))
        w2_scale = keep.tile([P, N], U8, name="w2_scale", align_bytes=64)
        nc.vector.memset(w2_scale[:].bitcast(I32), 0)
        for quadrant in range(4):
            rows = w2_scales[0, 4 * quadrant : 4 * quadrant + 4, :]
            nc.sync.dma_start(out=w2_scale[32 * quadrant : 32 * quadrant + 4, :].bitcast(I32), in_=rows.bitcast(I32))

        ident = keep.tile([P, P], F32, name="ident")
        make_identity(nc, ident[:])

        score_row = pair_table[0][:, HALF_T:T]
        nc.vector.tensor_copy(out=score_row[:, 0 : S // 2], in_=score_table.indirect(entries(0, 2)))
        nc.vector.tensor_copy(out=score_row[:, S // 2 : S], in_=tables[:, 0 : T + SPARE].indirect(entries(2, 4)))

        score_cols = [pair_table[1][:, TURNED : TURNED + BANK_BLOCKS], pair_table[1][:, HALF_T - BANK_BLOCKS : HALF_T]]
        scores = keep.tile([P, S], F32, name="scores")
        zeros = keep.tile([P, P], F32, name="zeros")
        nc.vector.memset(zeros[:], 0.0)
        score_bank = {}

        def turn_scores(q):
            bank = banks.tile([P, BANK_BLOCKS, P], F32, name="bank")
            for r in range(BANK_BLOCKS):
                b = BANK_BLOCKS * q + r
                nc.tensor.transpose(bank[:, r, :], score_row[:, P * b : P * (b + 1)], ident[:])
            nc.vector.tensor_copy(out=score_cols[q], in_=bank[:, :, P - 1])

        def spread_scores(q):
            score_bank[q] = score_banks.tile([P, BANK_BLOCKS, P], F32, name="score_bank")
            for r in range(BANK_BLOCKS):
                nc.tensor.transpose(score_bank[q][:, r, :], score_cols[q][:, r : r + 1].to_broadcast([P, P]), ident[:])

        def copy_scores(q):
            nc.scalar.copy(out=scores[:, S // 2 * q : S // 2 * (q + 1)], in_=score_bank[q][:].rearrange("p r n -> p (r n)"))

        x_quads0 = keep.tile([P, 2 * CHUNK], F32, name="x_quads0", align_bytes=64)
        x_quads3 = keep.tile([P, 2 * CHUNK], F32, name="x_quads3", align_bytes=64)
        x_quads = [x_quads0[:], w1_words[1][:, 0 : 2 * CHUNK], w1_words[1][:, 2 * CHUNK : 4 * CHUNK], x_quads3[:]]
        arena = keep.tile([P, PLACES * CHUNK], F32, name="arena")
        picked = arena[:].bitcast(U32)
        w1_bf16 = last[:].bitcast(BF16)

        def cast_x(load):
            pair, first, width, (a, b) = X_LOADS[load]
            rest = (b, width) if a == 0 else (0, a)
            for copy, (c0, c1) in ((nc.vector.tensor_copy, (a, b)), (nc.scalar.copy, rest)):
                if c0 < c1:
                    copy(
                        out=pair_table[pair][:, first + c0 : first + c1].bitcast(BF16).rearrange("p (c i j) -> p c j i", i=LINE, j=2),
                        in_=x_raw[load][:, :, c0:c1].rearrange("p j (c i) -> p c j i", i=LINE),
                    )

        def gather_first(pair):
            nc.vector.tensor_copy(
                out=x_quads[0].bitcast(U32).rearrange("p (n u) -> p n u", u=2)[:, :, pair],
                in_=pair_table[pair].bitcast(U32).indirect(entries(0, 1)),
            )

        def gather_x(window, c0, c1, place):
            nc.vector.tensor_copy(
                out=picked[:, CHUNK * place : CHUNK * (place + c1 - c0)],
                in_=window.bitcast(U32).indirect(entries(c0, c1)),
            )

        def weave(copy, chunk, place):
            first = chunk - 1
            words = picked[:, CHUNK * first : CHUNK * (2 * place - first)].rearrange("p (u n) -> p n u", u=2)
            copy(out=x_quads[chunk].bitcast(U32).rearrange("p (n u) -> p n u", u=2), in_=words[:, 0:CHUNK])

        def cast_w1(copy, half, t0, t1):
            copy(
                out=w1_bf16.rearrange("p (t m j) -> p m j t", t=PACK, j=PACK)[:, P // 2 * half : P // 2 * (half + 1), :, t0:t1],
                in_=w1_raw[half].rearrange("p j (m t) -> p m j t", t=PACK)[:, :, :, t0:t1],
            )

        x_codes = {}
        x_scale = {}

        def quantize_x(chunk, tag):
            codes = keep.tile([P, CHUNK], U32, name=f"x_codes{chunk}", tag=tag, align_bytes=64)
            scale = keep.tile([P, CHUNK], U8, name=f"x_scale{chunk}", align_bytes=64)
            nc.vector.quantize_mx(out=codes[:].bitcast(FP8X4), scales=scale[:], in_=x_quads[chunk].bitcast(BF16))
            x_codes[chunk] = codes[:, 0:CHUNK]
            x_scale[chunk] = scale[:, 0:CHUNK]

        w1_codes = keep.tile([P, H], U32, name="w1_codes", align_bytes=64)
        w1_scale = keep.tile([P, H], U8, name="w1_scale", align_bytes=64)

        def quantize_w1(t0, t1):
            nc.vector.quantize_mx(
                out=w1_codes[:, P * t0 : P * t1].bitcast(FP8X4),
                scales=w1_scale[:, P * t0 : P * t1],
                in_=w1_bf16[:, PACK * P * t0 : PACK * P * t1],
            )

        cast_x(0)
        warm_codes = keep.tile([P, max(WARM_PASSES)], U32, name="warm_codes", align_bytes=64)
        warm_scale = keep.tile([P, max(WARM_PASSES)], U8, name="warm_scale", align_bytes=64)
        nc.vector.quantize_mx(out=warm_codes[:].bitcast(FP8X4), scales=warm_scale[:], in_=pair_table[0][:, 0 : 2 * max(WARM_PASSES)].bitcast(BF16))
        for q in range(2):
            turn_scores(q)
        cast_x(1)
        for q in range(2):
            spread_scores(q)
        for q in range(2):
            copy_scores(q)
        gather_x(tables[:, T : 2 * T + HELD], 1, CHUNKS, 0)
        gather_first(0)
        for load in (2, 3, 4):
            cast_x(load)
        cast_w1(nc.scalar.copy, 0, 0, PACK // 2)
        cast_w1(nc.scalar.copy, 0, PACK // 2, PACK)
        warm_bank = score_banks.tile([P, BANK_BLOCKS, P], F32, name="score_bank")
        for r in range(WARM_DELAY):
            nc.tensor.transpose(warm_bank[:, r, :], w1_early[:, r * P : (r + 1) * P], ident[:])
        for width in WARM_PASSES:
            nc.tensor.matmul_mx(
                out=warm_bank[:].rearrange("p r n -> p (r n)")[:, 0:width],
                lhsT=warm_codes[:, 0:P].bitcast(FP8X4),
                lhsT_scale=warm_scale[:, 0:P],
                rhs=warm_codes[:, 0:width].bitcast(FP8X4),
                rhs_scale=warm_scale[:, 0:width],
                start=True,
                stop=True,
            )
        gather_first(1)
        gather_x(pair_table[1], 1, CHUNKS - 1, PAIR1_PLACE)
        cast_w1(nc.scalar.copy, 1, PACK // 2, PACK)
        cast_w1(nc.vector.tensor_copy, 1, 0, PACK // 2)
        quantize_x(0, "w1_early")
        quantize_w1(0, PACK // 2)
        weave(nc.scalar.copy, 1, PAIR1_PLACE)
        weave(nc.scalar.copy, 2, PAIR1_PLACE + 1)
        quantize_w1(PACK // 2, PACK)
        quantize_x(1, "x_codes1")
        gather_x(pair_table[1], CHUNKS - 1, CHUNKS, PAIR1_PLACE)
        quantize_x(2, "x_codes2")
        weave(nc.vector.tensor_copy, CHUNKS - 1, PAIR1_PLACE)

        h_bf16 = {}
        y_bank = {}
        y = {}

        def layer1(c):
            b0, b1 = PIECES[c]
            h_bf16[c] = keep.tile([P, PACK * P * (b1 - b0)], BF16, name=f"h_bf16_{c}", tag=f"h_codes{c - 2}", align_bytes=64)
            for b in range(b0, b1):
                chunk, s = divmod(b, CHUNK // P)
                bank = banks.tile([P, PACK, P], F32, name="bank")
                for t in range(PACK):
                    w_cols = slice(t * P, (t + 1) * P)
                    nc.tensor.matmul_mx(
                        out=bank[:, t, :],
                        lhsT=w1_codes[:, w_cols].bitcast(FP8X4),
                        lhsT_scale=w1_scale[:, w_cols],
                        rhs=x_codes[chunk][:, s * P : (s + 1) * P].bitcast(FP8X4),
                        rhs_scale=x_scale[chunk][:, s * P : (s + 1) * P],
                        start=True,
                        stop=True,
                    )
                nc.scalar.activation(
                    h_bf16[c][:, PACK * P * (b - b0) : PACK * P * (b - b0 + 1)].rearrange("p (n i t) -> p n t i", i=2, t=PACK),
                    bank[:].rearrange("p t (n i) -> p n t i", i=2),
                    SILU,
                )

        def layer2(c):
            width = P * (PIECES[c][1] - PIECES[c][0])
            h_codes = keep.tile([P, width], U32, name=f"h_codes{c}", tag=f"h_codes{c}", align_bytes=64)
            h_scale = keep.tile([P, width], U8, name=f"h_scale{c}", align_bytes=64)
            y_bank[c] = ybanks.tile([P, width], F32, name="y_bank")
            for first in range(0, width, CHUNK):
                end = min(first + CHUNK, width)
                nc.vector.quantize_mx(
                    out=h_codes[:, first:end].bitcast(FP8X4),
                    scales=h_scale[:, first:end],
                    in_=h_bf16[c][:, PACK * first : PACK * end],
                )
                nc.tensor.matmul_mx(
                    out=y_bank[c][:, first:end],
                    lhsT=w2_codes[:].bitcast(FP4X4),
                    lhsT_scale=w2_scale[:],
                    rhs=h_codes[:, first:end].bitcast(FP8X4),
                    rhs_scale=h_scale[:, first:end],
                    start=True,
                    stop=True,
                )
            y[c] = keep.tile([P, width], F32, name=f"y{c}")

        def places(c):
            return result[:].indirect(offsets[:, PIECES[c][0] * P // 16 : PIECES[c][1] * P // 16])

        def copy_y(c):
            nc.scalar.copy(out=y[c][:], in_=y_bank[c][:])

        def scatter(c):
            nc.vector.tensor_tensor(places(c), y[c][:], scores[:, P * PIECES[c][0] : P * PIECES[c][1]], MULT)

        layer1(0)
        layer2(0)
        quantize_x(CHUNKS - 1, "h_codes-2")
        nc.vector.tensor_tensor(y[0][:], y_bank[0][:], scores[:, 0:P], MULT)
        layer1(1)
        layer2(1)
        nc.vector.tensor_tensor(places(0), y[0][:], zeros[:], ADD)
        for c in range(2, len(PIECES)):
            layer1(c)
            copy_y(c - 1)
            layer2(c)
            scatter(c - 1)
        copy_y(len(PIECES) - 1)
        scatter(len(PIECES) - 1)
        nc.sync.dma_start(out=out, in_=result[:])
